import numpy as np
CORES = [2,10,18,26,34,42,50,58,66,74,82,90,98,106,114,122,130,138,146,154,162,170,178,186,194,202,210,218,226,234,242,250]
N = 32
T = 256
ROUTE = [[[2,21],[25,5],[16,9],[19,24],[5,21],[29,30],[11,1],[26,8],[19,20],[1,11],[26,30],[25,13],[28,8],[7,26],[19,18],[13,4],[6,19],[16,29],[8,25],[11,22],[7,5],[10,7],[31,7],[1,9],[2,17],[21,29],[31,30],[14,24],[23,15],[18,19],[26,2],[24,15],[26,12],[7,11],[25,7],[24,6],[24,21],[5,19],[20,31],[31,26],[5,15],[2,8],[20,31],[25,4],[21,29],[15,16],[0,4],[23,2],[21,15],[8,5],[15,29],[25,5],[13,20],[0,1],[26,24],[3,27],[8,12],[8,31],[16,28],[21,25],[16,9],[21,4],[23,0],[27,23],[5,2],[21,19],[17,22],[24,4],[2,10],[25,0],[18,14],[11,10],[21,23],[8,4],[13,19],[12,29],[22,10],[2,27],[5,1],[18,17],[12,21],[16,11],[11,2],[30,21],[24,23],[21,12],[11,29],[30,31],[14,21],[4,28],[3,16],[30,8],[25,7],[0,31],[21,18],[4,24],[15,16],[16,21],[1,5],[14,11],[25,23],[22,25],[20,22],[29,0],[0,17],[16,13],[7,18],[8,10],[15,3],[8,31],[31,8],[18,29],[17,28],[22,18],[7,20],[24,9],[0,9],[30,13],[20,4],[12,8],[2,6],[24,9],[20,24],[6,31],[21,20],[13,24],[3,20],[25,7],[22,12],[23,19],[0,7],[15,1],[24,14],[15,22],[28,26],[10,0],[5,6],[25,2],[28,9],[30,15],[0,28],[1,13],[2,22],[2,20],[1,11],[2,18],[7,13],[25,21],[11,1],[17,15],[8,26],[15,0],[12,17],[13,4],[11,30],[2,15],[13,25],[25,4],[11,9],[31,9],[18,2],[19,23],[16,23],[28,15],[0,22],[27,20],[23,14],[15,2],[19,22],[16,22],[17,30],[5,24],[14,30],[17,26],[17,23],[17,26],[14,5],[29,12],[3,26],[7,21],[25,0],[6,20],[23,31],[13,30],[31,28],[2,17],[2,12],[27,7],[26,0],[4,13],[25,13],[6,30],[31,29],[30,27],[15,13],[30,23],[19,12],[22,8],[8,30],[8,1],[19,29],[1,3],[4,30],[7,2],[5,15],[14,27],[26,12],[10,22],[23,5],[5,0],[16,10],[25,14],[25,26],[10,6],[15,31],[18,29],[22,23],[26,8],[31,11],[13,1],[19,11],[13,23],[25,0],[7,1],[21,17],[26,20],[23,9],[31,3],[30,10],[9,28],[3,2],[29,25],[10,22],[16,29],[15,6],[31,28],[29,1],[9,31],[10,11],[5,24],[8,10],[18,20],[23,8],[25,18],[19,30],[6,15],[14,22],[9,30],[26,14],[0,26],[8,18],[4,25],[13,18],[5,12],[20,18],[13,15]],[[25,18],[4,26],[17,13],[21,18],[0,11],[12,14],[31,2],[23,17],[29,10],[2,26],[12,21],[9,21],[9,7],[28,23],[22,30],[1,9],[17,21],[16,4],[30,5],[19,15],[6,10],[22,2],[1,23],[8,5],[26,15],[25,24],[15,11],[25,4],[0,5],[12,22],[12,5],[16,8],[10,28],[14,23],[28,11],[10,6],[12,9],[7,24],[26,29],[0,6],[14,9],[11,18],[28,8],[15,27],[31,10],[14,19],[13,7],[20,23],[1,13],[16,19],[10,6],[16,1],[23,15],[31,2],[19,20],[30,19],[11,10],[13,29],[12,20],[1,11],[19,26],[3,28],[13,27],[21,23],[31,27],[19,7],[21,12],[16,10],[17,6],[26,10],[3,16],[31,21],[10,8],[9,8],[24,2],[30,19],[1,31],[31,21],[1,8],[5,28],[25,24],[1,24],[18,19],[12,26],[3,30],[16,6],[31,25],[18,30],[12,22],[31,23],[22,0],[30,16],[0,3],[17,16],[9,24],[6,31],[23,27],[6,11],[14,9],[31,4],[9,17],[3,19],[3,24],[15,2],[26,9],[10,27],[14,20],[30,15],[22,24],[25,11],[31,28],[26,7],[20,18],[7,24],[8,23],[31,19],[28,14],[28,7],[6,29],[8,25],[15,8],[12,30],[21,10],[13,28],[9,18],[20,26],[15,5],[4,25],[27,11],[10,5],[12,26],[2,13],[23,29],[19,20],[15,2],[25,16],[1,10],[24,1],[19,18],[20,21],[6,9],[18,3],[18,9],[14,31],[22,18],[18,12],[25,21],[19,20],[8,19],[4,26],[18,1],[27,12],[2,11],[29,11],[3,5],[18,17],[25,15],[9,29],[25,24],[28,5],[22,31],[0,18],[22,7],[19,1],[6,19],[29,25],[3,22],[15,11],[16,25],[3,29],[6,1],[15,1],[24,29],[19,14],[27,25],[13,12],[19,25],[30,5],[20,9],[3,13],[5,2],[1,27],[29,9],[10,4],[1,27],[1,15],[16,5],[8,6],[27,7],[14,15],[18,16],[28,26],[6,20],[25,1],[28,7],[17,22],[21,15],[31,16],[5,6],[27,15],[23,17],[2,11],[15,7],[19,25],[28,18],[2,3],[6,18],[28,27],[20,2],[5,22],[15,27],[10,4],[5,14],[9,6],[4,6],[3,20],[17,15],[21,15],[14,24],[16,31],[6,0],[6,22],[20,17],[10,18],[16,17],[18,5],[11,4],[0,2],[29,22],[19,13],[4,9],[29,24],[14,9],[22,1],[24,1],[29,11],[5,3],[21,22],[21,12],[0,10],[26,1],[15,17],[8,4],[5,17],[12,8],[7,2],[31,11],[8,18],[26,1],[31,4],[4,18],[23,27],[16,29],[4,7],[11,14],[2,1]],[[18,0],[20,4],[2,9],[3,22],[22,0],[0,22],[22,11],[13,21],[27,1],[4,28],[8,21],[12,28],[18,26],[17,16],[11,21],[18,31],[11,12],[12,5],[5,9],[4,8],[14,31],[0,2],[10,29],[13,0],[8,4],[1,12],[3,21],[9,24],[5,18],[22,16],[10,30],[16,26],[19,6],[24,12],[26,27],[28,8],[18,26],[20,15],[28,17],[15,3],[10,4],[15,26],[26,8],[25,22],[13,5],[15,0],[24,9],[7,11],[0,31],[19,26],[25,17],[29,20],[12,30],[14,6],[1,21],[26,11],[16,27],[30,22],[27,14],[28,1],[0,15],[20,31],[4,11],[9,17],[3,20],[1,11],[2,4],[25,9],[22,23],[4,3],[2,30],[0,12],[18,16],[22,21],[9,5],[20,6],[21,15],[6,11],[22,21],[20,21],[6,7],[0,23],[27,14],[21,11],[5,20],[11,31],[9,3],[0,19],[9,7],[12,7],[3,6],[13,12],[21,10],[13,2],[27,3],[29,9],[7,13],[31,9],[0,3],[7,18],[26,25],[14,5],[17,30],[24,25],[11,31],[12,23],[18,25],[31,6],[21,11],[4,8],[8,18],[24,16],[23,21],[1,23],[30,28],[31,6],[5,27],[19,26],[23,12],[22,20],[22,3],[15,28],[7,15],[19,27],[7,21],[17,15],[2,31],[4,17],[30,10],[20,0],[27,30],[5,8],[18,24],[11,13],[9,14],[26,21],[17,3],[1,12],[23,14],[24,11],[8,6],[15,27],[1,11],[7,22],[27,26],[15,22],[6,16],[20,26],[10,23],[30,28],[19,6],[28,21],[1,4],[28,24],[23,9],[3,28],[22,0],[26,19],[5,26],[21,12],[2,0],[0,5],[27,18],[13,6],[20,8],[16,8],[5,25],[9,1],[4,18],[10,28],[10,27],[15,7],[17,23],[23,28],[22,24],[5,7],[16,20],[21,6],[7,8],[1,30],[31,9],[23,15],[13,28],[12,31],[2,23],[29,2],[28,31],[18,29],[17,22],[7,31],[30,5],[10,28],[17,21],[11,23],[27,11],[0,14],[1,6],[3,26],[12,8],[26,3],[1,17],[27,31],[1,8],[17,2],[2,30],[31,15],[7,14],[19,1],[27,1],[27,7],[14,22],[23,8],[15,28],[11,26],[1,16],[26,17],[10,19],[4,18],[22,14],[15,8],[11,8],[15,21],[3,8],[22,30],[18,15],[25,3],[28,26],[2,29],[24,31],[28,22],[9,14],[11,26],[6,7],[29,9],[30,24],[31,9],[2,3],[29,16],[12,22],[4,13],[5,17],[23,29],[21,22],[13,6],[11,3],[21,14],[23,2],[11,10],[5,22],[4,24],[16,25],[3,25],[29,8],[5,18],[28,10],[30,19]],[[16,0],[10,2],[31,22],[3,22],[9,3],[19,28],[25,0],[23,25],[27,15],[17,24],[19,6],[13,15],[24,9],[31,20],[13,4],[1,28],[4,18],[27,19],[15,13],[24,30],[27,12],[21,23],[26,22],[25,7],[13,15],[4,31],[19,13],[17,4],[8,28],[27,6],[7,21],[10,19],[15,24],[6,31],[17,0],[29,14],[31,6],[17,22],[30,12],[20,30],[21,31],[7,18],[25,29],[5,24],[4,2],[14,26],[26,25],[0,14],[22,19],[1,12],[30,11],[25,10],[18,17],[16,19],[4,15],[25,20],[12,15],[5,16],[12,31],[23,14],[31,21],[2,18],[31,18],[20,24],[28,3],[15,13],[2,14],[12,25],[29,2],[11,14],[2,4],[19,27],[16,23],[5,12],[15,6],[26,18],[28,3],[3,13],[5,9],[1,19],[11,7],[11,27],[8,16],[31,4],[17,3],[1,9],[3,8],[6,10],[30,4],[22,17],[10,26],[30,2],[29,4],[9,15],[18,24],[27,22],[28,21],[7,3],[20,6],[16,7],[17,4],[26,2],[16,0],[0,12],[9,20],[14,13],[13,21],[5,31],[10,3],[10,0],[26,31],[17,2],[19,27],[12,27],[21,24],[29,13],[27,13],[11,18],[6,11],[21,13],[0,18],[30,16],[23,12],[29,18],[18,11],[21,26],[30,19],[25,5],[16,20],[20,24],[25,30],[12,19],[24,16],[14,31],[18,2],[24,7],[24,0],[7,9],[18,5],[8,23],[11,17],[4,6],[10,8],[4,26],[3,31],[24,11],[19,31],[24,11],[22,26],[22,17],[1,5],[22,9],[29,7],[24,11],[30,7],[25,0],[20,19],[27,20],[12,5],[3,25],[20,1],[2,28],[21,26],[2,8],[12,22],[4,1],[29,10],[25,8],[17,28],[26,14],[13,8],[17,25],[18,22],[0,26],[23,24],[11,31],[27,7],[7,18],[11,29],[3,14],[16,18],[19,24],[25,10],[30,6],[30,3],[17,21],[9,25],[14,4],[13,30],[9,27],[28,4],[7,2],[20,16],[27,3],[19,25],[17,22],[25,7],[25,27],[19,8],[6,29],[27,24],[26,19],[20,21],[7,26],[18,2],[7,22],[9,28],[9,30],[4,13],[28,6],[25,15],[11,10],[9,13],[4,23],[22,18],[17,25],[2,8],[17,8],[22,10],[3,0],[29,9],[25,21],[1,31],[14,19],[10,17],[16,3],[18,25],[13,11],[20,10],[20,24],[21,17],[22,0],[25,16],[10,1],[8,24],[4,8],[22,26],[15,12],[1,31],[18,30],[17,0],[31,4],[17,23],[16,26],[22,18],[19,14],[15,1],[13,2],[25,6],[11,14],[18,31],[21,12],[10,14],[1,9],[30,21],[17,30]],[[0,5],[9,3],[7,10],[5,2],[11,21],[26,19],[29,20],[16,19],[16,20],[25,8],[17,19],[13,25],[2,11],[31,8],[5,13],[27,20],[25,0],[22,31],[10,21],[2,15],[13,15],[27,18],[10,7],[1,11],[18,31],[12,18],[10,16],[28,11],[10,11],[21,1],[16,13],[0,15],[10,25],[1,25],[0,31],[12,19],[3,24],[16,14],[24,16],[3,4],[19,3],[26,22],[19,22],[20,2],[27,7],[15,20],[22,11],[18,12],[18,23],[3,31],[12,19],[10,4],[13,7],[10,26],[27,30],[1,12],[4,0],[24,15],[9,5],[10,20],[19,25],[10,3],[6,0],[7,20],[16,6],[27,10],[7,13],[15,23],[6,19],[11,2],[24,26],[18,7],[5,13],[25,12],[13,30],[8,30],[0,24],[8,26],[12,25],[12,6],[25,12],[16,26],[29,9],[25,14],[18,0],[18,9],[13,30],[5,16],[2,8],[17,28],[31,29],[28,7],[2,17],[21,17],[22,26],[12,5],[23,20],[17,19],[4,30],[14,15],[17,31],[20,4],[15,17],[3,20],[8,27],[15,19],[9,13],[5,29],[2,23],[16,2],[9,21],[4,20],[24,13],[30,19],[18,23],[9,20],[30,3],[11,31],[30,5],[25,18],[16,28],[31,13],[26,5],[18,6],[5,17],[15,9],[17,19],[31,26],[28,4],[13,25],[7,4],[11,31],[10,20],[31,25],[18,7],[22,0],[9,14],[27,24],[0,27],[13,8],[21,28],[4,0],[26,8],[15,14],[8,0],[19,25],[29,4],[16,25],[23,26],[0,27],[11,5],[22,25],[4,17],[23,6],[0,18],[30,16],[29,14],[18,31],[17,5],[12,22],[1,15],[6,25],[18,20],[21,1],[13,7],[30,5],[9,7],[18,10],[16,4],[10,21],[19,8],[25,31],[30,8],[27,9],[11,8],[7,1],[28,27],[15,28],[24,7],[22,4],[7,13],[8,23],[28,31],[0,27],[15,0],[25,1],[25,31],[8,14],[6,28],[1,2],[20,14],[4,26],[2,15],[6,18],[19,8],[24,6],[14,13],[24,23],[6,30],[24,3],[24,26],[26,9],[11,6],[7,9],[27,8],[30,4],[25,1],[7,9],[9,23],[17,3],[17,7],[1,30],[19,20],[19,14],[27,6],[1,8],[2,21],[2,19],[6,20],[28,0],[8,27],[19,9],[11,0],[26,21],[13,10],[31,7],[15,11],[17,19],[28,23],[29,30],[17,13],[10,6],[6,27],[6,28],[5,18],[9,19],[11,25],[19,26],[20,29],[23,19],[8,23],[14,5],[23,3],[13,25],[16,18],[24,18],[4,24],[7,16],[20,30],[17,13],[0,28],[8,29],[24,20],[22,15],[4,12],[6,7]],[[6,26],[12,7],[18,23],[7,22],[10,22],[10,16],[26,16],[21,7],[7,19],[5,23],[26,12],[6,0],[19,3],[10,15],[0,23],[24,29],[16,24],[31,21],[25,2],[4,3],[31,28],[13,30],[5,25],[16,0],[2,4],[26,24],[15,0],[9,24],[13,22],[0,28],[0,18],[17,16],[10,3],[2,25],[21,10],[11,29],[10,18],[7,19],[10,27],[8,16],[17,22],[18,23],[21,23],[14,5],[1,28],[16,25],[3,28],[24,6],[23,24],[8,16],[5,14],[0,29],[2,14],[21,8],[25,31],[14,5],[10,9],[18,23],[29,27],[14,9],[20,13],[1,2],[11,13],[31,2],[17,14],[10,7],[27,6],[13,22],[2,24],[23,18],[22,17],[1,27],[9,15],[10,20],[18,2],[27,31],[13,3],[20,9],[31,20],[27,30],[28,21],[5,12],[21,18],[29,24],[15,2],[3,18],[21,16],[25,4],[3,22],[16,19],[27,2],[20,24],[5,1],[7,27],[23,5],[24,5],[0,10],[6,26],[13,17],[20,3],[17,27],[16,21],[10,15],[29,26],[29,9],[7,1],[27,2],[4,11],[1,23],[5,3],[11,27],[20,6],[3,23],[21,29],[1,2],[28,19],[1,10],[25,24],[14,12],[10,7],[16,10],[25,7],[2,21],[28,5],[10,3],[30,11],[4,25],[10,22],[30,5],[23,12],[14,4],[25,24],[26,12],[6,20],[11,15],[13,4],[9,30],[29,1],[12,27],[25,23],[15,19],[10,14],[4,22],[5,14],[31,9],[8,22],[4,9],[21,8],[2,4],[1,18],[29,9],[1,9],[9,15],[18,14],[15,1],[25,1],[15,9],[15,11],[29,22],[1,21],[2,27],[26,2],[8,26],[18,26],[27,13],[15,19],[15,14],[25,2],[19,2],[28,19],[10,4],[11,20],[6,14],[15,21],[6,27],[29,27],[27,4],[25,14],[2,25],[31,21],[22,14],[2,25],[20,26],[7,3],[24,11],[19,7],[3,11],[13,21],[20,8],[24,13],[3,23],[31,7],[15,29],[28,30],[23,4],[22,14],[19,26],[26,6],[24,14],[2,28],[27,13],[5,29],[11,18],[16,31],[0,22],[14,25],[28,20],[21,12],[26,0],[19,15],[23,29],[13,31],[13,12],[30,28],[10,21],[30,7],[12,6],[26,0],[13,8],[17,7],[20,6],[26,30],[5,27],[30,20],[2,18],[31,11],[3,18],[1,3],[10,25],[20,8],[26,7],[16,0],[30,23],[4,26],[18,29],[9,26],[19,4],[24,26],[30,12],[21,28],[14,13],[28,25],[7,23],[28,5],[16,11],[23,9],[26,9],[7,31],[18,14],[29,20],[6,12],[16,26],[6,0],[0,18],[8,0],[29,17]],[[2,8],[27,3],[18,26],[1,13],[27,17],[11,28],[8,4],[22,18],[24,23],[12,10],[4,29],[7,18],[23,26],[11,22],[27,10],[9,1],[4,13],[9,26],[0,2],[16,14],[16,3],[3,2],[15,12],[29,26],[22,17],[26,18],[16,26],[30,0],[1,3],[20,0],[14,7],[4,13],[31,17],[24,7],[0,17],[10,28],[10,13],[26,13],[21,22],[18,27],[12,1],[19,6],[14,20],[5,19],[13,25],[3,19],[29,10],[8,11],[2,15],[29,28],[11,15],[11,14],[18,30],[24,29],[24,8],[5,16],[30,7],[7,18],[24,3],[25,18],[23,10],[15,19],[15,17],[25,18],[10,28],[29,8],[17,12],[0,25],[26,16],[29,23],[6,27],[22,8],[21,20],[17,30],[0,5],[25,14],[27,12],[8,16],[22,16],[31,10],[13,2],[22,9],[27,22],[24,1],[23,29],[22,2],[13,10],[30,6],[31,20],[21,24],[11,9],[1,21],[15,23],[23,14],[17,18],[26,14],[21,22],[21,8],[30,12],[29,30],[0,17],[22,2],[17,26],[1,4],[4,3],[30,22],[1,16],[7,0],[7,17],[12,9],[19,3],[8,17],[28,9],[28,5],[20,28],[27,19],[25,16],[5,28],[0,20],[0,26],[7,19],[27,13],[8,23],[30,18],[9,13],[29,6],[9,18],[1,20],[28,14],[31,11],[3,10],[9,5],[17,18],[15,1],[17,22],[6,13],[16,2],[25,16],[17,30],[4,14],[18,6],[28,19],[31,0],[14,8],[20,3],[2,14],[19,18],[7,9],[4,1],[30,6],[7,26],[30,28],[25,10],[7,9],[9,27],[25,14],[7,26],[26,2],[17,2],[24,31],[3,10],[18,15],[21,10],[0,14],[10,2],[25,19],[11,22],[5,4],[18,20],[25,5],[8,0],[19,12],[12,24],[16,19],[14,13],[7,18],[28,17],[4,8],[29,13],[26,25],[14,10],[3,6],[0,1],[2,15],[26,1],[21,23],[3,21],[23,29],[17,24],[31,26],[11,7],[11,31],[8,29],[13,31],[17,21],[16,4],[29,25],[15,31],[0,6],[1,9],[0,24],[9,23],[9,3],[11,6],[26,10],[23,16],[31,27],[5,10],[9,3],[10,5],[7,14],[15,25],[2,0],[29,25],[19,17],[2,15],[29,21],[8,1],[3,30],[4,15],[5,31],[29,13],[9,25],[22,16],[10,21],[18,30],[11,14],[22,6],[21,27],[20,28],[16,12],[30,15],[20,15],[23,22],[16,1],[27,21],[22,14],[1,17],[25,22],[21,9],[11,22],[30,11],[0,24],[19,24],[22,6],[21,4],[1,26],[1,4],[0,29],[22,15],[29,14],[31,11],[12,18],[1,20],[28,21],[0,4]],[[3,9],[2,27],[23,21],[28,6],[29,8],[12,15],[29,22],[19,1],[7,26],[23,2],[31,30],[24,15],[29,14],[8,3],[1,29],[15,7],[10,25],[25,16],[5,7],[4,25],[19,12],[9,11],[21,8],[31,18],[10,26],[15,31],[1,0],[29,4],[29,9],[13,21],[14,28],[28,22],[1,20],[27,25],[9,5],[4,7],[31,12],[24,5],[31,3],[1,18],[18,31],[16,11],[26,5],[18,14],[5,7],[24,10],[24,21],[26,11],[14,5],[8,1],[26,7],[20,10],[13,17],[21,23],[29,16],[30,19],[12,6],[1,21],[13,28],[9,23],[31,1],[15,23],[0,22],[11,1],[5,29],[30,28],[9,6],[31,8],[30,14],[0,2],[14,28],[21,24],[29,6],[5,12],[17,6],[29,4],[1,5],[1,22],[2,4],[30,26],[6,17],[11,29],[5,24],[21,9],[12,7],[25,0],[5,7],[1,22],[2,16],[20,25],[23,29],[20,29],[2,23],[3,19],[30,13],[12,19],[6,22],[23,30],[11,15],[28,10],[6,26],[10,17],[28,16],[20,15],[1,24],[5,29],[11,29],[24,11],[26,7],[26,7],[12,18],[29,7],[11,18],[12,19],[18,24],[0,3],[18,8],[11,17],[20,25],[24,2],[17,15],[29,12],[23,9],[18,19],[5,2],[19,2],[12,20],[14,7],[6,20],[20,3],[9,3],[11,20],[0,13],[10,25],[30,27],[1,25],[26,31],[4,12],[2,15],[25,12],[27,14],[1,26],[24,7],[14,5],[24,23],[3,6],[26,9],[19,5],[20,14],[19,17],[8,13],[29,15],[2,3],[9,15],[29,15],[6,18],[14,5],[6,12],[13,1],[27,11],[17,9],[8,26],[18,9],[16,28],[29,25],[10,15],[4,11],[19,10],[25,3],[5,19],[10,3],[13,28],[0,27],[5,6],[4,1],[24,27],[19,6],[13,25],[22,21],[0,14],[6,13],[6,12],[27,0],[8,12],[15,18],[1,12],[13,8],[2,13],[18,7],[5,0],[26,18],[23,1],[17,19],[24,6],[6,29],[22,9],[12,19],[14,0],[22,28],[27,13],[17,5],[20,6],[28,17],[15,8],[19,12],[7,19],[8,31],[21,13],[13,14],[24,10],[5,20],[13,15],[24,14],[27,4],[16,17],[8,2],[7,28],[2,12],[17,8],[19,13],[21,29],[22,12],[10,17],[22,24],[26,25],[29,1],[24,30],[1,31],[6,17],[31,2],[4,29],[30,1],[21,30],[17,12],[13,20],[26,5],[18,3],[11,20],[8,7],[26,3],[1,22],[1,0],[18,21],[11,7],[2,5],[25,3],[4,27],[28,18],[25,10],[0,30],[4,7],[10,19],[0,27],[9,14],[21,0],[31,3]],[[18,28],[4,10],[2,27],[26,17],[13,28],[5,20],[24,29],[22,9],[3,18],[17,25],[18,17],[28,29],[10,0],[6,13],[17,11],[10,16],[17,12],[7,3],[1,30],[13,27],[15,30],[17,16],[14,2],[25,0],[16,1],[14,12],[27,20],[29,4],[7,31],[11,20],[16,10],[29,16],[17,0],[14,20],[7,23],[11,22],[30,18],[1,15],[8,29],[2,14],[3,1],[25,22],[10,4],[27,20],[9,30],[31,14],[5,28],[31,6],[17,20],[7,30],[1,2],[12,31],[13,0],[7,11],[5,24],[20,10],[0,30],[7,16],[29,8],[21,15],[15,23],[18,3],[31,8],[16,25],[14,13],[28,24],[15,3],[19,22],[21,7],[30,16],[9,27],[9,22],[8,19],[20,26],[3,21],[24,22],[11,13],[8,19],[4,7],[9,5],[16,13],[18,5],[8,18],[0,25],[27,1],[19,12],[31,15],[31,3],[0,27],[14,12],[21,11],[9,3],[15,19],[17,3],[9,28],[28,4],[16,13],[19,31],[14,13],[2,26],[14,24],[12,27],[19,23],[9,0],[21,23],[15,24],[11,29],[28,15],[21,25],[4,11],[13,25],[0,26],[26,25],[11,0],[11,6],[31,20],[9,31],[30,13],[28,19],[23,24],[0,31],[11,29],[27,3],[30,27],[13,29],[19,7],[23,6],[31,12],[31,27],[26,17],[9,24],[24,2],[26,14],[21,30],[21,16],[30,13],[19,28],[9,13],[26,24],[13,0],[23,24],[22,5],[20,24],[24,14],[12,26],[7,24],[25,12],[23,14],[13,1],[11,26],[17,6],[19,31],[6,0],[30,11],[16,14],[18,30],[12,28],[14,23],[9,5],[10,23],[25,4],[23,13],[27,1],[18,13],[5,22],[6,28],[15,29],[10,7],[23,10],[22,7],[26,20],[11,19],[2,13],[15,12],[1,24],[26,4],[3,26],[25,29],[18,12],[21,20],[11,30],[4,17],[25,4],[21,11],[13,25],[31,5],[21,11],[9,2],[27,22],[10,2],[31,25],[27,11],[3,30],[12,5],[21,1],[24,10],[5,23],[23,16],[20,29],[13,29],[29,11],[1,20],[24,29],[10,26],[17,3],[0,18],[30,20],[5,15],[24,5],[18,24],[19,2],[13,28],[15,13],[11,15],[9,12],[17,21],[22,30],[16,12],[10,25],[6,3],[6,29],[10,8],[28,31],[6,18],[30,21],[27,10],[20,10],[11,9],[5,13],[20,17],[8,25],[10,31],[16,25],[23,21],[25,27],[20,4],[21,6],[17,29],[23,25],[23,10],[10,17],[15,7],[6,2],[30,20],[11,18],[10,16],[27,2],[21,15],[5,11],[18,21],[5,8],[9,16],[7,27],[14,17],[20,0],[17,28]],[[2,29],[23,9],[31,3],[9,24],[14,7],[18,17],[6,26],[3,23],[31,6],[13,18],[2,7],[12,31],[14,11],[11,28],[28,17],[18,25],[15,12],[17,21],[24,17],[25,14],[6,14],[13,14],[29,16],[29,10],[9,23],[15,20],[24,6],[4,10],[28,7],[20,28],[25,23],[18,16],[0,13],[1,0],[29,13],[8,1],[14,3],[10,21],[16,14],[24,21],[12,6],[13,22],[19,18],[8,13],[9,28],[11,9],[12,6],[20,16],[3,27],[27,14],[3,2],[3,2],[24,12],[15,3],[23,12],[12,8],[17,13],[9,20],[29,4],[22,18],[13,29],[0,25],[24,11],[14,12],[21,16],[19,18],[16,14],[27,15],[26,31],[31,11],[27,26],[19,27],[21,18],[11,10],[23,4],[31,25],[22,3],[7,12],[1,11],[31,0],[11,1],[30,22],[29,13],[27,29],[26,6],[31,3],[23,15],[15,6],[19,18],[30,3],[17,14],[0,4],[18,4],[2,3],[1,18],[1,29],[27,16],[8,17],[23,7],[28,30],[23,19],[14,23],[31,13],[20,30],[23,11],[26,2],[6,9],[21,2],[22,5],[16,7],[10,9],[10,1],[6,2],[27,3],[24,11],[30,3],[24,13],[5,8],[21,30],[15,8],[10,23],[27,26],[13,2],[10,18],[4,10],[23,28],[27,9],[15,25],[28,30],[10,6],[18,0],[10,31],[12,25],[22,11],[12,11],[28,3],[6,31],[25,21],[30,11],[15,25],[26,13],[31,11],[26,14],[3,1],[19,29],[3,30],[29,9],[20,29],[24,23],[10,14],[3,8],[15,25],[28,14],[11,13],[19,22],[13,22],[15,24],[30,4],[21,19],[4,30],[31,3],[27,4],[0,8],[6,15],[30,11],[26,8],[26,18],[10,3],[14,20],[2,23],[18,31],[13,18],[26,7],[28,18],[5,17],[3,31],[11,30],[21,15],[0,3],[19,11],[4,22],[3,15],[22,28],[5,20],[3,20],[15,5],[16,7],[9,3],[30,1],[19,12],[1,3],[8,18],[13,31],[19,8],[9,10],[2,30],[0,30],[30,29],[2,13],[5,13],[6,17],[8,9],[11,1],[19,24],[7,13],[2,12],[30,5],[3,28],[13,7],[6,10],[15,22],[4,18],[4,19],[31,11],[28,18],[15,0],[2,16],[29,31],[5,18],[30,27],[19,23],[9,13],[29,22],[7,17],[11,8],[16,2],[23,29],[21,25],[27,10],[31,26],[28,5],[17,5],[14,2],[8,1],[5,8],[10,4],[26,25],[4,15],[24,10],[13,8],[21,29],[27,21],[20,18],[13,8],[27,14],[24,0],[5,6],[7,4],[11,20],[30,3],[11,5],[15,16],[18,9],[20,13],[22,25],[5,13]],[[31,26],[18,28],[4,30],[26,30],[16,12],[11,0],[23,30],[31,19],[7,8],[13,6],[18,5],[27,19],[1,21],[9,26],[8,27],[1,31],[9,27],[28,27],[25,18],[5,18],[25,12],[14,27],[18,25],[23,20],[24,31],[10,15],[22,13],[30,21],[29,21],[28,23],[25,17],[11,13],[14,4],[11,21],[15,19],[11,25],[9,27],[24,28],[10,29],[22,0],[12,26],[24,8],[10,29],[22,4],[16,20],[19,24],[17,3],[1,14],[3,1],[31,12],[25,24],[6,25],[17,11],[18,14],[14,16],[23,12],[6,18],[11,29],[24,5],[1,30],[0,6],[22,5],[24,14],[9,22],[8,18],[20,6],[10,1],[17,0],[8,18],[10,17],[27,1],[19,14],[14,20],[27,5],[10,22],[1,3],[2,1],[7,26],[19,14],[14,7],[12,31],[18,22],[24,27],[31,16],[17,31],[14,10],[22,16],[24,10],[5,20],[28,21],[18,16],[6,27],[0,30],[0,16],[18,2],[9,30],[1,6],[15,5],[27,1],[24,27],[18,23],[4,23],[15,3],[8,30],[30,23],[20,21],[20,13],[11,24],[26,20],[20,9],[2,9],[19,9],[29,12],[5,0],[26,15],[25,15],[24,6],[18,25],[4,1],[30,14],[9,30],[17,3],[9,19],[23,13],[13,1],[21,28],[1,10],[21,12],[30,19],[26,21],[4,7],[17,8],[26,11],[14,16],[28,15],[29,20],[23,19],[15,4],[4,5],[29,17],[26,3],[16,10],[11,21],[8,28],[8,1],[9,2],[25,22],[7,23],[18,1],[26,2],[26,12],[15,22],[29,17],[27,20],[24,26],[10,18],[24,14],[3,24],[16,2],[28,11],[18,4],[29,23],[0,9],[19,17],[0,13],[21,11],[20,16],[25,16],[31,30],[26,18],[0,22],[25,3],[31,12],[28,14],[0,11],[0,18],[24,3],[6,0],[2,10],[25,15],[0,5],[4,17],[6,8],[14,8],[9,12],[29,8],[27,10],[28,27],[26,2],[26,27],[28,6],[13,29],[10,2],[26,31],[1,10],[13,3],[22,24],[6,11],[22,27],[0,8],[10,18],[20,9],[27,0],[25,19],[27,24],[20,12],[14,5],[27,3],[18,31],[24,7],[23,5],[12,2],[7,24],[18,30],[23,1],[30,11],[6,14],[11,0],[2,17],[13,16],[24,27],[7,16],[21,18],[4,23],[27,18],[24,27],[30,1],[12,20],[11,16],[0,27],[24,11],[30,16],[28,26],[27,17],[2,17],[15,8],[17,29],[22,13],[23,18],[7,19],[26,27],[10,7],[13,0],[20,17],[23,1],[3,31],[9,17],[13,14],[8,28],[30,8],[15,20],[0,18],[0,8],[22,13],[17,12],[17,31]],[[11,13],[15,28],[6,8],[18,22],[0,27],[31,3],[28,18],[0,29],[15,23],[26,5],[8,12],[21,2],[25,29],[16,26],[2,19],[14,12],[26,5],[28,26],[24,28],[5,11],[16,7],[27,13],[14,31],[0,5],[19,29],[9,25],[7,6],[0,30],[1,18],[21,2],[4,28],[31,24],[2,21],[11,27],[19,23],[0,24],[1,2],[4,6],[6,10],[6,20],[17,1],[26,19],[0,11],[13,17],[28,10],[3,16],[27,28],[14,19],[21,9],[25,21],[6,27],[24,22],[2,3],[27,0],[23,24],[0,7],[0,20],[19,13],[12,21],[27,20],[27,23],[16,1],[20,13],[15,4],[9,5],[30,9],[31,19],[10,23],[11,15],[31,10],[9,18],[13,22],[6,29],[30,15],[2,12],[3,22],[21,15],[7,9],[25,29],[6,9],[27,8],[14,20],[5,1],[21,24],[8,10],[10,3],[22,7],[17,3],[22,31],[21,7],[3,21],[4,23],[0,23],[7,8],[2,12],[6,31],[20,9],[13,14],[18,27],[18,21],[22,29],[6,8],[18,1],[18,20],[11,10],[14,8],[12,15],[4,9],[15,28],[0,31],[29,12],[4,26],[5,30],[19,1],[24,18],[2,23],[8,7],[21,26],[15,8],[23,28],[4,2],[2,30],[15,29],[3,5],[10,11],[0,17],[0,26],[5,2],[1,3],[10,25],[1,16],[12,0],[6,18],[8,3],[21,11],[7,27],[13,28],[16,24],[30,24],[6,24],[16,11],[12,31],[8,19],[17,4],[29,30],[27,14],[20,17],[23,6],[31,6],[9,12],[10,14],[14,18],[29,11],[29,0],[20,29],[27,22],[28,30],[3,18],[13,11],[12,7],[6,31],[20,3],[20,11],[31,27],[7,25],[9,1],[23,28],[4,12],[7,12],[15,7],[24,25],[0,5],[21,6],[8,27],[20,24],[24,5],[31,14],[26,3],[29,30],[31,24],[19,28],[26,9],[10,0],[10,6],[1,21],[5,31],[14,20],[13,3],[13,15],[19,6],[26,4],[6,11],[24,21],[17,28],[6,7],[31,20],[0,14],[27,25],[15,26],[10,2],[20,1],[18,24],[9,14],[21,3],[16,1],[0,14],[18,8],[12,11],[31,2],[15,25],[11,20],[17,19],[1,20],[13,15],[19,31],[28,14],[29,17],[22,3],[8,7],[9,16],[6,5],[4,18],[20,10],[21,12],[30,20],[14,20],[4,16],[3,9],[10,28],[25,28],[13,28],[6,28],[25,16],[19,14],[21,29],[22,2],[12,19],[6,26],[7,2],[30,27],[3,1],[1,26],[13,27],[8,21],[16,2],[23,17],[7,24],[8,20],[8,5],[7,20],[15,17],[24,11],[13,4],[1,18],[11,8],[6,5]],[[10,29],[16,8],[12,28],[14,17],[13,3],[0,2],[14,13],[30,17],[6,3],[10,13],[19,21],[16,0],[5,22],[28,10],[16,25],[27,6],[11,26],[17,13],[7,5],[4,8],[10,20],[4,27],[20,21],[4,11],[24,17],[24,10],[17,10],[10,14],[19,3],[22,2],[8,10],[24,29],[30,18],[15,14],[12,3],[25,18],[18,15],[4,21],[7,25],[17,8],[19,2],[2,21],[16,23],[13,16],[15,3],[17,19],[26,5],[3,29],[28,22],[14,22],[27,9],[13,18],[24,6],[16,21],[30,18],[11,6],[27,20],[3,24],[5,24],[18,7],[12,27],[21,4],[23,29],[20,31],[21,18],[2,12],[29,5],[4,6],[12,24],[1,2],[6,16],[26,23],[21,8],[21,31],[2,9],[4,31],[31,24],[15,23],[5,24],[30,29],[16,25],[19,30],[6,15],[24,6],[26,7],[6,11],[8,12],[1,26],[16,11],[19,16],[3,4],[20,28],[12,28],[9,26],[18,19],[4,7],[16,18],[28,22],[3,0],[21,23],[24,6],[18,26],[13,16],[10,4],[18,8],[6,23],[27,10],[7,22],[7,12],[1,16],[27,11],[13,9],[16,17],[0,16],[13,19],[5,30],[14,17],[19,7],[12,29],[29,27],[21,4],[19,9],[15,14],[12,8],[15,23],[28,22],[16,0],[3,11],[21,16],[6,28],[18,21],[21,3],[12,28],[5,31],[0,18],[16,25],[2,27],[14,1],[2,25],[24,1],[25,20],[1,7],[30,23],[31,3],[22,29],[9,3],[20,18],[21,7],[23,21],[18,30],[16,3],[3,16],[11,12],[15,5],[27,18],[2,30],[13,1],[14,9],[4,27],[13,20],[13,5],[15,21],[11,9],[22,16],[26,4],[7,3],[14,8],[20,9],[28,11],[10,20],[24,9],[2,24],[5,8],[6,1],[13,12],[14,18],[5,8],[14,0],[2,20],[31,13],[22,12],[14,29],[28,18],[9,10],[17,27],[0,28],[29,8],[9,18],[29,20],[9,26],[1,20],[14,19],[1,24],[28,6],[8,17],[22,0],[5,21],[29,1],[6,28],[29,7],[11,27],[23,8],[4,13],[3,30],[11,9],[28,1],[25,6],[3,31],[30,23],[30,15],[0,29],[5,26],[17,18],[12,26],[15,23],[25,6],[27,26],[24,27],[19,18],[10,2],[20,13],[2,20],[31,13],[27,23],[19,9],[26,6],[4,19],[9,4],[9,18],[0,23],[26,11],[0,8],[4,27],[27,20],[2,27],[19,17],[14,3],[26,29],[7,10],[6,25],[24,9],[19,23],[25,11],[29,16],[19,12],[10,25],[24,16],[21,16],[20,30],[24,28],[17,26],[29,25],[30,24],[25,6],[5,8],[11,0]],[[8,29],[27,0],[31,0],[23,9],[6,14],[3,15],[10,7],[14,26],[12,18],[17,26],[26,24],[27,10],[22,31],[3,12],[11,20],[20,12],[31,25],[27,29],[17,10],[14,6],[24,20],[12,1],[23,11],[10,29],[8,22],[17,24],[23,6],[11,15],[4,13],[23,31],[3,4],[12,6],[22,31],[3,2],[28,31],[29,26],[25,9],[0,25],[5,3],[10,6],[21,3],[15,19],[29,17],[4,15],[18,20],[21,13],[11,17],[29,16],[23,19],[19,16],[22,16],[4,22],[7,3],[31,20],[26,16],[15,18],[11,17],[26,2],[24,15],[26,29],[28,23],[4,26],[21,30],[3,19],[27,14],[21,9],[30,28],[2,25],[13,22],[28,31],[12,2],[28,5],[19,20],[20,31],[14,21],[7,8],[18,5],[8,17],[12,2],[16,11],[28,27],[21,15],[5,14],[21,12],[24,10],[19,31],[11,13],[12,8],[9,11],[24,18],[16,7],[30,5],[12,6],[27,24],[16,0],[16,7],[14,12],[15,7],[13,2],[18,16],[25,11],[12,4],[4,1],[24,29],[9,22],[17,22],[17,14],[25,28],[8,16],[19,27],[27,17],[23,8],[1,15],[25,28],[27,21],[24,3],[18,9],[8,26],[11,28],[15,22],[4,27],[29,18],[28,4],[1,2],[23,0],[6,3],[17,14],[11,18],[0,31],[18,12],[21,29],[21,31],[11,4],[2,19],[7,6],[22,25],[2,5],[2,12],[9,14],[24,8],[24,16],[26,22],[24,10],[19,9],[12,27],[19,29],[5,1],[8,26],[3,5],[7,22],[25,8],[3,17],[22,9],[15,20],[26,25],[2,29],[21,12],[18,9],[14,11],[15,3],[5,26],[8,5],[13,30],[1,11],[14,30],[16,28],[7,29],[2,11],[12,2],[14,23],[9,26],[23,19],[6,23],[0,23],[9,3],[10,19],[30,5],[6,31],[20,24],[26,16],[2,25],[7,23],[17,15],[8,5],[12,4],[22,28],[7,23],[17,14],[17,26],[4,21],[28,8],[20,4],[9,23],[6,20],[25,19],[31,3],[22,28],[23,16],[29,24],[2,8],[14,1],[30,5],[27,2],[19,9],[5,7],[17,12],[8,27],[1,2],[18,25],[14,27],[11,24],[18,4],[8,1],[10,13],[12,28],[9,2],[20,9],[13,0],[26,28],[4,12],[26,13],[21,9],[16,6],[4,2],[12,14],[17,13],[2,24],[12,10],[10,30],[21,26],[25,30],[25,5],[27,6],[12,19],[20,13],[19,14],[26,29],[1,21],[29,1],[18,13],[19,2],[24,11],[20,5],[6,10],[8,28],[8,6],[22,11],[14,4],[5,9],[26,20],[10,31],[14,10],[6,28],[1,13],[28,17],[10,5]],[[29,15],[6,17],[0,5],[10,2],[8,23],[6,0],[24,13],[16,12],[18,17],[28,8],[9,3],[24,27],[19,21],[16,11],[31,28],[21,25],[2,27],[30,5],[20,1],[29,25],[2,3],[0,26],[14,13],[24,22],[4,1],[31,24],[4,29],[5,15],[6,15],[16,5],[1,28],[3,30],[18,12],[7,16],[21,29],[25,9],[23,9],[14,6],[2,31],[2,12],[6,20],[15,13],[24,5],[7,26],[2,23],[9,4],[8,22],[7,2],[20,30],[23,21],[5,15],[17,3],[1,4],[29,5],[14,11],[24,0],[0,26],[21,28],[7,18],[14,27],[13,26],[30,9],[14,18],[1,6],[31,2],[28,24],[24,14],[11,31],[16,17],[16,19],[31,4],[12,23],[23,22],[6,8],[19,25],[5,4],[0,7],[31,20],[2,29],[4,14],[29,1],[2,8],[29,6],[5,29],[31,19],[17,19],[2,18],[4,8],[1,11],[29,25],[2,15],[18,17],[11,30],[19,29],[7,15],[28,16],[19,14],[4,9],[1,13],[8,29],[5,17],[15,17],[10,3],[15,6],[26,22],[9,30],[18,28],[28,26],[2,7],[16,7],[0,26],[9,27],[12,0],[14,24],[30,26],[12,6],[27,18],[24,19],[9,15],[2,8],[10,14],[19,9],[10,1],[24,30],[25,20],[27,4],[23,3],[3,20],[12,2],[7,1],[14,2],[24,21],[11,8],[4,9],[19,17],[7,21],[24,4],[17,29],[17,5],[16,25],[30,7],[9,17],[0,17],[2,11],[13,5],[10,3],[21,5],[7,17],[24,0],[17,15],[14,20],[10,30],[29,21],[24,0],[8,15],[26,7],[5,12],[4,1],[14,23],[29,3],[14,11],[27,28],[11,23],[16,27],[25,7],[10,31],[28,30],[22,13],[21,2],[14,4],[0,18],[6,15],[29,15],[10,31],[13,22],[4,31],[0,1],[9,11],[7,22],[18,8],[18,3],[14,24],[1,18],[2,13],[23,6],[10,5],[12,31],[18,24],[17,24],[19,21],[17,13],[4,31],[19,6],[11,18],[30,1],[30,11],[19,10],[2,12],[5,21],[3,1],[20,30],[22,7],[18,16],[6,9],[26,10],[5,16],[4,5],[21,30],[9,28],[21,8],[15,12],[30,19],[29,16],[0,2],[5,26],[29,8],[28,14],[6,19],[14,1],[21,22],[29,18],[5,30],[22,15],[22,18],[7,10],[27,0],[23,13],[30,16],[18,22],[28,24],[12,23],[2,30],[26,23],[14,4],[17,7],[5,19],[24,18],[20,6],[16,6],[7,10],[28,22],[19,11],[0,12],[19,12],[27,29],[2,18],[18,2],[24,16],[6,12],[9,12],[25,7],[3,14],[31,26],[12,17],[5,6],[23,26]],[[9,21],[13,12],[30,29],[3,5],[29,2],[26,29],[20,15],[0,2],[23,10],[18,27],[29,6],[6,5],[21,11],[9,21],[23,13],[10,9],[30,5],[8,2],[24,22],[25,5],[17,3],[20,28],[5,0],[17,4],[25,7],[1,13],[2,15],[7,22],[3,23],[3,9],[0,3],[21,26],[18,5],[2,13],[24,13],[27,30],[27,19],[1,25],[9,11],[15,29],[15,2],[16,30],[14,16],[9,4],[10,7],[29,5],[12,23],[27,11],[26,25],[23,27],[5,15],[7,3],[22,6],[26,16],[20,9],[25,29],[31,15],[3,17],[3,8],[30,15],[0,7],[22,15],[29,1],[19,7],[12,27],[0,2],[21,28],[17,25],[12,2],[12,24],[21,4],[9,4],[3,25],[2,8],[17,22],[2,30],[4,21],[23,4],[21,0],[11,5],[2,12],[21,23],[3,10],[5,0],[31,7],[10,3],[26,31],[19,5],[2,29],[24,16],[28,1],[24,11],[26,2],[20,15],[8,3],[8,14],[2,12],[8,28],[10,17],[30,16],[27,19],[20,23],[13,0],[31,0],[31,20],[22,2],[6,25],[27,28],[21,8],[16,0],[29,15],[0,29],[10,28],[21,23],[17,21],[7,6],[6,26],[18,4],[20,22],[25,16],[8,14],[21,23],[21,18],[5,12],[23,12],[24,26],[26,18],[1,29],[28,13],[11,10],[27,6],[20,15],[7,30],[27,15],[2,1],[20,15],[19,12],[24,1],[11,15],[2,10],[0,21],[14,15],[26,1],[19,15],[2,19],[4,15],[29,12],[30,24],[12,21],[12,24],[24,17],[7,9],[20,8],[1,13],[13,31],[20,31],[11,22],[25,13],[14,27],[18,20],[24,17],[11,9],[14,6],[15,30],[19,28],[18,19],[26,6],[14,28],[29,22],[1,29],[0,5],[8,5],[14,6],[17,21],[19,17],[9,22],[29,1],[5,6],[15,18],[14,0],[28,3],[0,27],[6,18],[3,28],[27,25],[14,29],[26,28],[0,17],[27,19],[9,3],[17,12],[13,17],[10,6],[0,9],[29,23],[23,25],[2,0],[20,22],[16,13],[16,15],[28,21],[20,29],[11,1],[0,16],[6,30],[10,15],[25,30],[30,19],[12,16],[11,3],[17,27],[29,10],[29,16],[10,25],[4,12],[3,30],[0,26],[17,0],[5,22],[9,15],[2,0],[29,30],[26,29],[8,31],[28,12],[26,4],[18,4],[13,2],[2,14],[24,17],[20,12],[0,19],[13,11],[11,15],[26,28],[1,30],[1,24],[21,3],[15,1],[24,0],[25,10],[23,18],[30,19],[26,28],[12,1],[5,20],[13,4],[7,17],[21,13],[21,29],[14,3],[9,3],[12,10],[17,29],[29,23],[5,30]],[[24,4],[26,23],[3,25],[17,5],[2,22],[13,27],[26,1],[30,4],[29,18],[10,1],[3,4],[29,27],[2,29],[6,9],[6,4],[30,7],[21,7],[15,26],[6,7],[29,30],[20,31],[14,10],[17,30],[10,7],[1,3],[28,18],[26,6],[4,18],[15,0],[30,29],[23,3],[9,10],[4,20],[31,16],[31,27],[15,4],[12,2],[29,5],[6,28],[1,29],[17,9],[27,4],[27,11],[5,27],[26,14],[20,30],[27,19],[5,23],[8,29],[14,16],[21,13],[6,2],[5,11],[8,18],[29,19],[21,20],[25,10],[8,24],[22,26],[14,1],[0,12],[26,0],[16,31],[20,0],[4,8],[15,0],[29,12],[11,28],[0,22],[1,18],[4,11],[28,22],[23,26],[29,31],[18,2],[12,4],[25,16],[2,23],[16,3],[21,19],[1,16],[9,27],[17,13],[30,25],[31,9],[4,24],[21,25],[27,28],[16,9],[26,23],[19,28],[12,17],[6,2],[2,1],[31,22],[0,16],[9,2],[7,21],[25,13],[15,13],[25,9],[12,3],[7,24],[19,16],[30,11],[6,21],[4,8],[0,21],[10,22],[26,14],[28,11],[9,28],[18,0],[23,10],[14,13],[22,18],[15,22],[18,0],[1,17],[17,22],[12,18],[26,31],[17,27],[22,20],[7,10],[7,17],[12,13],[14,15],[13,29],[5,18],[20,10],[23,22],[28,23],[9,8],[9,22],[29,5],[24,19],[27,28],[17,19],[31,25],[5,7],[3,29],[9,15],[5,12],[20,10],[25,23],[9,1],[4,13],[20,27],[28,2],[17,16],[13,18],[30,23],[14,28],[25,28],[11,10],[2,19],[19,2],[9,20],[11,21],[31,22],[29,28],[9,2],[15,30],[26,3],[1,11],[12,17],[22,13],[24,18],[24,2],[2,20],[26,4],[22,25],[13,14],[28,19],[24,15],[19,23],[26,7],[4,26],[4,12],[29,17],[8,2],[13,23],[14,10],[12,1],[0,14],[15,16],[6,19],[15,27],[27,17],[19,3],[12,8],[11,2],[13,11],[28,21],[29,0],[9,15],[7,19],[21,7],[14,0],[11,22],[6,1],[23,2],[11,4],[18,8],[0,9],[19,16],[14,28],[25,22],[29,10],[19,20],[6,25],[9,7],[17,16],[25,0],[6,16],[24,29],[13,10],[30,28],[22,23],[0,3],[27,31],[23,6],[23,18],[16,27],[20,3],[25,29],[20,2],[18,13],[24,20],[9,25],[16,1],[30,19],[8,2],[27,5],[7,23],[8,0],[5,25],[23,19],[10,23],[2,8],[30,0],[7,21],[22,27],[26,12],[7,10],[19,23],[21,16],[30,15],[30,23],[12,0],[9,2],[8,6],[26,1],[7,4],[27,30]],[[30,7],[23,12],[30,20],[11,24],[13,3],[27,21],[31,8],[17,8],[5,11],[15,23],[30,18],[20,15],[30,19],[3,0],[4,8],[5,10],[27,20],[9,31],[6,13],[9,23],[9,4],[6,27],[5,18],[11,18],[28,23],[16,27],[28,6],[10,30],[22,30],[1,13],[0,3],[3,13],[19,31],[1,4],[26,6],[11,9],[0,1],[24,25],[31,16],[16,6],[3,5],[19,2],[27,18],[21,11],[7,23],[4,13],[0,2],[13,28],[11,2],[7,21],[2,14],[1,23],[19,1],[18,23],[8,13],[27,8],[10,25],[27,12],[29,31],[27,2],[9,1],[0,15],[5,20],[23,4],[6,31],[28,20],[3,0],[9,2],[18,0],[4,12],[0,8],[6,19],[12,31],[10,25],[17,26],[22,31],[4,24],[21,4],[16,29],[19,23],[0,24],[24,22],[18,7],[26,30],[8,22],[28,25],[27,14],[30,1],[23,9],[23,11],[21,19],[20,25],[25,24],[3,30],[9,23],[7,15],[11,9],[16,31],[14,21],[28,9],[8,17],[30,25],[1,22],[2,4],[6,3],[16,23],[16,1],[0,12],[27,7],[8,2],[19,6],[25,1],[29,16],[5,19],[5,20],[14,15],[20,21],[15,0],[19,18],[30,2],[19,2],[9,28],[10,25],[19,3],[28,24],[28,18],[1,17],[18,23],[25,4],[16,19],[18,21],[14,29],[15,23],[21,28],[23,10],[3,5],[6,22],[24,15],[26,12],[4,25],[5,20],[30,27],[4,7],[6,9],[14,30],[5,22],[28,13],[7,26],[24,10],[14,24],[29,12],[4,10],[14,7],[17,30],[2,16],[7,26],[6,20],[0,22],[13,2],[29,14],[27,12],[10,4],[6,2],[7,18],[15,21],[3,12],[18,3],[24,16],[28,16],[12,23],[10,28],[24,20],[15,18],[14,12],[3,1],[24,17],[14,22],[20,2],[3,28],[17,22],[30,20],[1,20],[12,29],[21,30],[30,6],[28,30],[29,10],[27,21],[17,31],[18,26],[30,19],[0,6],[6,20],[16,26],[30,21],[12,3],[19,30],[13,27],[10,23],[24,20],[19,28],[29,8],[1,17],[27,29],[1,31],[3,27],[7,6],[23,25],[21,20],[16,19],[9,0],[4,17],[2,3],[4,13],[6,15],[1,17],[22,6],[5,2],[26,1],[2,10],[20,13],[2,21],[13,16],[12,21],[7,27],[5,3],[29,17],[7,6],[30,12],[4,19],[10,22],[8,10],[28,4],[22,9],[10,23],[25,21],[2,21],[7,18],[0,31],[22,31],[15,10],[12,28],[11,18],[3,17],[6,31],[3,31],[24,27],[4,26],[29,26],[16,17],[6,0],[18,3],[24,11],[13,28],[22,27],[31,22]],[[16,3],[0,5],[12,13],[2,7],[12,30],[22,31],[0,14],[31,29],[13,20],[5,22],[21,31],[30,4],[27,24],[25,17],[24,18],[31,26],[15,31],[17,5],[31,26],[13,7],[13,22],[7,24],[23,31],[14,21],[22,0],[11,15],[21,20],[14,10],[9,21],[7,9],[16,15],[18,21],[14,2],[16,4],[2,9],[19,11],[6,29],[16,20],[26,23],[1,13],[24,18],[4,9],[11,15],[13,16],[26,12],[4,7],[6,12],[31,16],[31,19],[7,5],[5,4],[7,10],[31,23],[31,21],[15,16],[9,7],[9,17],[17,12],[9,4],[0,21],[21,16],[17,19],[8,6],[17,28],[3,21],[9,24],[8,15],[17,30],[31,26],[26,20],[24,2],[17,1],[23,22],[25,27],[31,7],[30,12],[23,13],[11,18],[10,29],[1,26],[8,13],[30,9],[30,10],[27,13],[5,27],[18,30],[18,25],[28,25],[21,5],[9,18],[30,2],[29,27],[9,2],[20,4],[26,31],[5,24],[27,19],[13,9],[19,8],[7,10],[18,6],[1,9],[19,3],[6,4],[30,19],[11,6],[25,14],[24,30],[28,22],[22,4],[0,22],[26,14],[9,14],[9,13],[5,8],[3,20],[21,27],[23,3],[4,20],[22,7],[25,5],[9,6],[3,23],[11,26],[10,20],[24,1],[13,18],[0,5],[19,0],[20,24],[18,31],[8,2],[5,28],[28,15],[7,14],[16,25],[3,25],[15,2],[28,1],[19,30],[1,2],[14,23],[5,9],[18,19],[13,8],[9,29],[14,20],[17,23],[28,21],[13,17],[15,0],[18,5],[31,22],[21,9],[13,21],[11,18],[17,1],[28,14],[17,0],[24,14],[10,11],[0,13],[29,16],[28,31],[3,21],[3,13],[19,20],[2,11],[20,9],[4,22],[26,2],[17,6],[7,24],[23,6],[27,25],[11,18],[3,30],[25,8],[23,15],[15,3],[24,23],[8,11],[5,12],[29,15],[12,28],[13,24],[8,21],[21,22],[8,26],[17,12],[31,8],[5,14],[6,4],[23,7],[15,29],[23,6],[24,22],[22,13],[10,6],[25,15],[22,12],[0,29],[4,25],[20,8],[22,25],[5,8],[2,31],[14,13],[22,21],[1,8],[5,23],[14,13],[30,6],[23,14],[9,25],[9,21],[15,14],[12,26],[16,3],[10,13],[4,8],[20,21],[6,22],[12,14],[20,29],[16,4],[27,17],[10,0],[21,5],[8,7],[6,13],[20,29],[31,21],[3,14],[6,28],[14,11],[4,11],[18,27],[17,5],[9,19],[12,30],[3,24],[24,9],[30,1],[1,20],[25,31],[26,2],[13,9],[26,22],[26,27],[26,4],[28,18],[7,22],[29,30],[16,28],[16,21]],[[2,26],[27,10],[11,14],[15,13],[0,1],[30,8],[16,21],[23,29],[22,27],[21,10],[15,20],[15,1],[0,16],[23,10],[24,5],[13,31],[23,14],[8,28],[15,4],[8,28],[14,28],[19,26],[22,11],[21,10],[5,24],[0,12],[6,30],[19,4],[25,11],[22,1],[22,24],[0,19],[4,10],[28,3],[13,14],[22,15],[5,14],[5,13],[28,19],[20,15],[21,9],[25,24],[12,14],[2,11],[9,17],[15,27],[30,27],[4,15],[2,0],[15,21],[17,6],[22,3],[31,19],[7,15],[9,27],[7,27],[26,21],[3,18],[20,2],[1,24],[1,23],[5,6],[27,6],[11,7],[9,14],[2,14],[11,17],[21,18],[28,19],[15,20],[8,23],[1,27],[27,30],[9,16],[16,13],[17,1],[26,4],[20,3],[8,7],[18,0],[30,26],[2,0],[31,13],[31,19],[13,30],[10,7],[26,14],[29,15],[15,12],[9,16],[14,20],[15,24],[3,15],[27,15],[27,13],[28,4],[4,22],[11,13],[5,18],[3,16],[2,15],[16,23],[19,16],[3,24],[6,29],[1,18],[14,31],[1,23],[1,2],[21,6],[1,11],[4,10],[21,31],[6,11],[17,27],[17,21],[22,20],[13,24],[4,2],[15,6],[0,8],[1,2],[12,11],[14,24],[24,18],[15,6],[7,3],[18,8],[1,25],[0,8],[16,30],[17,10],[25,27],[29,14],[11,31],[31,19],[3,19],[31,28],[8,13],[15,6],[29,12],[20,24],[31,20],[3,23],[15,28],[9,3],[30,20],[25,9],[0,4],[18,13],[30,3],[1,27],[3,28],[4,23],[8,31],[9,28],[29,20],[12,29],[24,15],[14,22],[29,0],[8,16],[3,0],[21,22],[17,11],[9,11],[11,20],[5,23],[18,27],[29,26],[23,25],[18,26],[19,10],[25,15],[20,13],[25,7],[12,18],[29,27],[18,2],[10,15],[31,7],[3,29],[23,2],[25,19],[22,7],[1,15],[5,17],[18,2],[30,3],[4,3],[8,23],[15,13],[20,28],[10,12],[22,5],[3,29],[12,9],[26,25],[2,3],[25,8],[25,23],[12,16],[7,22],[16,25],[23,31],[8,15],[24,23],[5,14],[28,11],[6,17],[4,1],[20,8],[22,13],[28,1],[17,20],[21,3],[24,22],[2,8],[17,0],[23,30],[9,14],[30,14],[27,23],[2,23],[7,18],[9,0],[2,29],[28,24],[12,16],[5,8],[2,3],[17,13],[18,22],[27,7],[15,7],[11,8],[6,16],[29,7],[29,28],[25,10],[25,3],[0,21],[27,18],[8,30],[29,26],[31,5],[24,18],[6,3],[11,4],[7,6],[9,26],[16,23],[24,4],[23,1],[15,6],[22,23]],[[27,16],[6,21],[30,9],[21,12],[25,29],[17,11],[5,6],[23,20],[19,5],[0,2],[11,20],[20,11],[4,15],[5,4],[2,23],[9,20],[17,13],[30,5],[17,8],[8,16],[7,10],[10,17],[12,21],[19,23],[6,10],[30,5],[5,11],[13,14],[16,26],[30,9],[0,25],[21,19],[1,0],[8,29],[20,22],[16,29],[7,2],[20,15],[9,26],[10,17],[4,26],[14,4],[25,14],[10,23],[28,14],[8,7],[4,0],[17,14],[19,26],[21,13],[24,10],[30,8],[17,2],[12,30],[4,28],[29,19],[1,2],[24,0],[1,31],[28,31],[2,10],[15,30],[22,31],[24,17],[14,1],[25,18],[26,25],[26,25],[24,6],[19,21],[10,4],[11,17],[1,28],[10,22],[31,6],[10,21],[0,6],[15,13],[8,11],[15,9],[29,26],[10,1],[23,25],[17,24],[16,1],[23,16],[17,22],[17,31],[22,29],[17,31],[10,0],[31,8],[28,24],[17,13],[6,26],[21,7],[22,23],[29,9],[18,28],[15,29],[2,0],[31,12],[29,26],[4,28],[16,24],[25,12],[6,13],[28,19],[7,25],[4,16],[31,9],[13,18],[31,20],[30,9],[22,7],[29,4],[9,2],[25,15],[24,13],[7,12],[3,14],[11,1],[5,14],[28,16],[0,1],[17,11],[13,19],[13,12],[3,29],[4,10],[13,7],[23,1],[16,15],[13,19],[28,16],[11,14],[3,26],[9,7],[19,9],[5,0],[0,9],[21,20],[16,18],[18,5],[6,4],[7,25],[29,15],[25,14],[8,29],[6,21],[30,7],[6,0],[12,2],[4,10],[20,0],[12,27],[14,5],[30,18],[4,25],[18,2],[10,15],[9,15],[12,7],[12,23],[4,21],[9,31],[12,8],[11,12],[16,10],[31,6],[29,17],[14,17],[1,14],[31,26],[17,0],[0,14],[24,15],[21,17],[26,12],[17,1],[16,2],[19,29],[30,26],[3,26],[29,20],[23,22],[10,4],[21,6],[26,9],[6,20],[0,24],[1,9],[26,14],[19,3],[23,11],[31,10],[15,21],[7,17],[25,10],[23,18],[16,13],[2,24],[14,20],[27,19],[9,4],[4,27],[19,7],[23,14],[21,17],[17,29],[29,22],[10,25],[31,8],[23,2],[5,26],[0,18],[30,23],[16,2],[5,0],[24,19],[26,18],[12,7],[24,18],[21,17],[2,5],[2,5],[23,14],[12,28],[21,10],[16,1],[22,3],[11,4],[4,29],[4,14],[18,0],[20,28],[7,19],[15,7],[15,1],[24,13],[18,3],[21,11],[3,24],[5,8],[10,7],[2,10],[2,17],[10,29],[5,24],[1,4],[12,16],[14,8],[13,15],[21,10],[4,11],[0,8]],[[22,14],[17,9],[24,19],[14,9],[20,8],[14,5],[2,7],[0,14],[20,11],[7,30],[12,9],[16,8],[25,0],[22,8],[5,11],[16,18],[16,5],[9,19],[30,29],[26,17],[28,25],[14,6],[9,10],[6,8],[27,16],[0,24],[4,7],[11,9],[15,22],[30,29],[11,18],[21,10],[22,1],[6,17],[21,17],[26,28],[22,12],[2,20],[2,1],[22,13],[21,0],[27,20],[31,0],[25,27],[1,14],[6,11],[15,25],[23,17],[19,17],[25,7],[30,12],[4,22],[5,2],[24,31],[8,25],[18,9],[28,31],[25,19],[17,15],[2,16],[21,17],[28,7],[0,5],[11,4],[7,16],[27,26],[13,17],[27,7],[30,21],[27,19],[27,2],[25,16],[15,25],[13,15],[21,17],[12,17],[14,2],[16,29],[16,8],[16,6],[0,19],[9,17],[8,23],[15,21],[18,14],[24,18],[0,9],[7,28],[20,18],[10,22],[21,0],[8,7],[11,15],[22,15],[18,10],[23,6],[11,31],[8,18],[24,13],[27,13],[6,29],[1,10],[26,22],[22,25],[12,31],[29,12],[19,9],[30,6],[13,4],[4,6],[27,3],[16,28],[20,31],[30,1],[6,28],[0,13],[25,19],[5,15],[29,6],[5,7],[0,15],[29,25],[28,25],[17,8],[17,31],[29,4],[29,12],[25,1],[10,23],[1,16],[9,24],[11,23],[3,11],[28,27],[25,23],[27,10],[19,7],[18,6],[16,31],[28,19],[4,2],[29,22],[14,25],[17,0],[25,22],[8,20],[16,21],[13,21],[27,23],[5,10],[14,15],[5,31],[31,12],[8,6],[12,14],[28,7],[13,11],[11,23],[21,1],[13,20],[13,29],[24,29],[4,15],[18,23],[28,6],[19,18],[20,30],[23,25],[19,30],[16,31],[13,2],[28,17],[31,18],[29,17],[17,24],[25,23],[10,16],[4,2],[31,14],[29,17],[25,31],[31,12],[13,1],[20,13],[29,3],[17,25],[29,15],[20,4],[14,4],[13,30],[2,19],[2,20],[31,9],[15,14],[16,31],[5,0],[0,18],[28,25],[9,1],[10,27],[17,13],[17,19],[18,19],[21,0],[20,3],[28,6],[6,23],[18,15],[26,12],[27,3],[0,2],[21,12],[12,11],[10,30],[10,28],[8,24],[14,18],[10,30],[10,30],[15,0],[19,15],[19,16],[25,16],[10,1],[25,2],[28,2],[19,9],[30,1],[21,14],[12,13],[9,24],[21,4],[7,15],[20,10],[10,28],[16,7],[21,7],[23,24],[26,0],[8,15],[20,29],[20,18],[18,15],[21,1],[0,4],[31,9],[12,19],[11,7],[22,24],[26,22],[28,9],[1,23],[11,18],[27,12],[29,18],[20,31]],[[17,19],[0,5],[19,21],[26,6],[8,18],[22,6],[30,0],[12,17],[21,22],[9,12],[11,1],[26,25],[11,16],[18,12],[6,2],[29,7],[0,12],[17,22],[25,19],[12,30],[14,1],[17,24],[31,11],[23,3],[7,23],[5,26],[6,17],[23,28],[10,24],[5,24],[22,26],[12,11],[13,20],[4,1],[17,13],[4,17],[26,20],[11,20],[1,7],[31,14],[29,13],[16,14],[14,17],[24,2],[11,29],[30,29],[1,31],[9,0],[5,1],[16,22],[26,19],[2,15],[4,16],[1,7],[1,11],[17,21],[23,0],[6,24],[31,7],[5,23],[22,6],[12,17],[27,25],[0,21],[6,16],[7,18],[10,21],[23,5],[5,30],[17,5],[13,23],[18,23],[7,8],[21,19],[31,19],[6,22],[18,6],[28,4],[20,0],[6,29],[8,16],[27,5],[14,31],[16,22],[9,23],[5,4],[24,12],[16,18],[20,23],[5,27],[29,23],[30,6],[27,29],[15,20],[1,29],[2,27],[31,2],[22,7],[12,19],[6,7],[24,25],[5,7],[23,2],[24,17],[24,8],[23,21],[24,14],[13,23],[11,6],[30,11],[20,0],[16,3],[3,21],[19,18],[11,4],[15,9],[19,6],[20,7],[1,12],[17,27],[5,31],[2,13],[15,18],[3,29],[19,17],[27,7],[14,20],[15,23],[29,16],[27,17],[6,0],[21,17],[30,26],[25,29],[30,4],[13,18],[28,12],[4,1],[7,4],[22,17],[14,13],[28,21],[4,24],[11,28],[16,13],[6,23],[29,9],[9,13],[13,6],[15,3],[15,13],[28,18],[19,16],[15,9],[18,14],[20,26],[2,31],[19,15],[22,21],[17,28],[23,17],[22,8],[21,9],[10,7],[6,10],[5,18],[31,29],[7,18],[25,17],[22,26],[13,10],[25,5],[15,28],[8,20],[26,11],[16,10],[3,1],[11,20],[7,9],[1,29],[11,18],[8,9],[26,23],[14,4],[30,26],[15,30],[23,31],[19,20],[23,31],[29,16],[18,29],[1,9],[18,20],[22,28],[21,8],[12,6],[19,4],[3,27],[6,10],[6,2],[22,13],[26,15],[20,6],[15,28],[22,5],[28,7],[28,0],[26,29],[6,21],[19,4],[31,27],[21,19],[16,2],[23,29],[7,9],[13,20],[6,12],[19,17],[23,16],[27,31],[5,31],[6,15],[2,29],[25,4],[2,1],[13,22],[21,8],[18,8],[29,14],[21,15],[22,6],[27,25],[23,30],[23,13],[16,21],[23,27],[5,1],[15,20],[6,5],[13,28],[6,21],[16,13],[12,3],[16,21],[31,28],[18,30],[20,5],[3,16],[12,11],[1,20],[26,23],[11,25],[25,27],[25,22],[21,28],[26,14]],[[22,11],[23,3],[22,15],[25,1],[0,16],[14,2],[17,15],[5,11],[17,22],[18,0],[14,9],[10,17],[13,8],[6,3],[27,19],[7,16],[12,28],[26,6],[1,5],[6,13],[25,31],[4,6],[15,18],[12,14],[0,2],[24,9],[14,1],[6,24],[1,27],[13,24],[3,7],[27,17],[9,17],[5,23],[9,13],[18,12],[11,4],[6,19],[17,11],[10,29],[19,20],[6,14],[19,16],[26,16],[5,6],[25,22],[6,7],[14,28],[28,10],[14,8],[29,10],[24,23],[14,21],[30,17],[6,2],[27,21],[9,1],[27,5],[10,9],[14,17],[10,28],[26,14],[28,17],[30,1],[5,11],[18,10],[11,9],[15,21],[19,11],[23,1],[29,16],[31,13],[13,26],[15,23],[10,30],[4,14],[24,29],[1,21],[23,16],[27,26],[22,9],[20,15],[25,15],[13,25],[6,24],[17,4],[22,8],[7,16],[24,3],[17,6],[24,9],[14,29],[22,3],[20,13],[3,28],[2,1],[20,26],[28,31],[10,23],[31,24],[15,2],[16,15],[25,5],[3,26],[1,27],[3,31],[20,31],[6,0],[27,28],[24,2],[20,29],[16,6],[14,1],[0,1],[31,22],[3,21],[4,20],[31,23],[24,23],[11,2],[5,6],[1,24],[25,15],[0,18],[24,31],[1,20],[21,19],[27,26],[15,21],[29,11],[1,15],[9,28],[1,6],[2,1],[14,0],[7,9],[10,23],[9,26],[14,31],[21,27],[26,11],[17,25],[6,23],[6,2],[14,2],[6,12],[17,18],[14,15],[3,15],[25,7],[12,14],[9,29],[10,6],[16,23],[2,10],[5,0],[23,19],[11,18],[5,19],[25,19],[13,4],[22,29],[21,2],[10,31],[22,9],[23,6],[0,13],[1,21],[11,3],[19,15],[31,27],[14,17],[17,18],[21,0],[24,31],[5,25],[19,0],[23,31],[1,29],[24,25],[1,15],[16,4],[1,28],[1,13],[29,27],[30,0],[16,20],[27,9],[28,13],[4,27],[2,18],[10,3],[7,16],[30,16],[6,1],[9,26],[13,14],[21,4],[15,11],[0,4],[12,15],[28,30],[24,17],[2,9],[13,1],[4,10],[4,6],[8,2],[16,15],[16,4],[0,22],[29,20],[5,10],[30,20],[11,22],[18,0],[3,19],[20,24],[30,24],[28,21],[7,30],[15,19],[17,28],[10,20],[0,25],[9,18],[11,28],[31,25],[14,22],[1,5],[1,9],[8,9],[2,15],[9,6],[17,3],[5,15],[8,4],[1,22],[27,14],[29,17],[30,17],[14,19],[25,3],[19,28],[11,14],[2,4],[13,26],[24,4],[24,17],[5,6],[20,25],[18,1],[13,23],[9,12],[5,20],[8,22]],[[10,9],[11,12],[14,17],[8,12],[1,8],[23,8],[17,24],[12,22],[31,11],[25,12],[23,26],[16,18],[30,20],[7,21],[19,0],[17,22],[13,12],[8,19],[18,11],[13,7],[14,24],[9,20],[27,4],[28,22],[14,9],[27,21],[26,29],[27,28],[10,17],[2,26],[20,25],[10,3],[24,10],[18,5],[0,18],[23,16],[31,16],[26,22],[18,28],[30,15],[30,9],[18,29],[30,21],[21,16],[8,1],[13,3],[14,25],[21,23],[4,5],[9,0],[3,14],[21,6],[31,12],[4,21],[11,8],[7,13],[5,30],[17,10],[25,24],[2,29],[2,12],[5,4],[20,24],[10,7],[0,5],[18,17],[8,6],[20,9],[23,30],[9,20],[10,24],[17,2],[22,8],[22,14],[22,29],[15,6],[29,10],[18,19],[19,22],[8,5],[11,3],[19,17],[26,29],[17,25],[3,0],[4,9],[29,10],[29,9],[18,28],[17,28],[23,14],[22,3],[26,14],[9,5],[9,27],[23,20],[27,5],[16,6],[24,16],[13,25],[27,31],[30,17],[6,1],[0,26],[3,15],[31,0],[6,10],[30,26],[9,14],[10,18],[31,6],[30,3],[8,9],[28,12],[25,9],[31,8],[23,24],[5,10],[28,1],[31,3],[30,8],[8,6],[30,10],[22,15],[25,8],[27,22],[16,9],[9,4],[21,13],[6,22],[24,27],[9,13],[28,17],[22,11],[11,4],[23,31],[30,26],[8,4],[12,2],[0,11],[31,28],[21,19],[20,10],[23,0],[5,31],[21,2],[5,31],[24,10],[29,2],[18,14],[20,28],[11,27],[0,14],[8,7],[19,22],[31,12],[3,10],[21,18],[2,26],[18,29],[23,7],[21,24],[31,20],[24,25],[5,1],[24,25],[1,26],[16,5],[15,13],[4,9],[17,19],[22,19],[29,28],[24,28],[17,13],[8,4],[7,3],[23,22],[12,23],[14,6],[25,19],[9,17],[20,11],[22,21],[13,12],[2,9],[22,0],[10,25],[19,18],[3,30],[30,23],[8,0],[9,14],[10,21],[12,26],[9,27],[8,25],[26,6],[19,17],[0,15],[13,10],[15,18],[28,9],[1,11],[23,3],[10,30],[31,27],[6,10],[8,21],[16,9],[16,18],[21,6],[5,0],[12,16],[22,24],[29,12],[7,1],[19,29],[3,19],[13,29],[25,1],[11,29],[31,9],[9,16],[4,20],[9,12],[1,15],[25,10],[18,20],[0,21],[13,27],[1,9],[24,22],[30,24],[14,4],[20,10],[3,23],[12,13],[12,3],[22,29],[10,20],[10,15],[24,30],[31,2],[12,25],[21,20],[17,23],[4,1],[29,18],[29,27],[6,9],[29,8],[11,8],[29,8],[12,26],[25,4]],[[7,6],[8,4],[21,23],[17,14],[21,19],[14,1],[24,5],[4,15],[27,26],[23,17],[28,20],[15,1],[12,7],[16,11],[9,14],[28,31],[14,24],[8,9],[3,25],[22,24],[15,26],[19,3],[14,27],[3,10],[21,7],[27,15],[14,27],[20,14],[8,11],[25,10],[23,4],[0,22],[8,7],[2,13],[6,16],[10,23],[11,12],[14,12],[15,18],[30,23],[8,18],[23,20],[18,7],[18,15],[7,20],[21,3],[25,26],[16,5],[9,2],[18,9],[11,13],[18,2],[19,13],[27,15],[31,20],[3,29],[30,2],[6,11],[2,15],[6,21],[5,27],[31,14],[21,13],[31,19],[10,20],[2,6],[11,15],[14,21],[14,28],[0,21],[1,10],[14,20],[18,30],[10,6],[27,30],[2,28],[7,31],[10,22],[9,3],[14,1],[31,21],[25,27],[21,13],[10,16],[10,4],[24,5],[14,22],[22,17],[19,23],[5,19],[26,16],[6,29],[5,23],[4,14],[13,1],[11,31],[28,12],[10,9],[16,14],[21,25],[28,0],[13,18],[24,27],[6,2],[11,5],[17,9],[5,16],[22,26],[12,16],[26,1],[17,13],[14,7],[27,10],[30,25],[6,4],[21,25],[12,4],[24,3],[4,10],[30,24],[22,25],[19,6],[21,10],[17,4],[23,0],[9,23],[0,20],[28,15],[5,13],[25,4],[21,31],[30,26],[26,5],[31,19],[14,25],[8,26],[5,12],[12,0],[14,4],[0,29],[10,23],[30,26],[28,8],[19,30],[20,25],[3,30],[18,17],[6,9],[31,6],[9,11],[13,19],[17,27],[13,22],[22,2],[2,15],[24,19],[29,2],[12,5],[17,15],[11,21],[9,16],[10,27],[27,2],[5,17],[21,0],[29,1],[20,27],[4,7],[12,20],[16,5],[21,2],[21,27],[26,2],[25,21],[18,28],[7,2],[7,5],[6,11],[25,18],[9,17],[25,16],[21,27],[9,25],[13,14],[30,24],[19,8],[27,9],[7,6],[21,25],[17,12],[21,10],[10,22],[17,27],[19,8],[1,25],[12,23],[25,7],[18,29],[9,13],[25,10],[20,7],[17,14],[19,15],[3,16],[11,16],[18,8],[19,31],[6,8],[25,27],[30,28],[20,17],[8,7],[10,18],[21,11],[16,7],[16,31],[10,16],[3,14],[5,19],[20,0],[10,19],[12,24],[13,31],[25,15],[21,7],[30,8],[6,22],[30,24],[15,31],[1,8],[17,13],[13,26],[20,27],[1,8],[26,0],[22,10],[22,28],[30,19],[28,9],[7,8],[16,12],[25,19],[9,18],[31,3],[7,15],[1,29],[23,3],[20,16],[6,29],[24,26],[17,20],[29,30],[28,12],[11,25],[24,2],[11,30]],[[13,12],[6,8],[15,1],[30,9],[29,3],[18,25],[7,14],[21,22],[12,11],[18,1],[23,4],[0,20],[21,12],[21,17],[25,21],[18,31],[23,31],[4,26],[2,9],[13,6],[2,23],[24,3],[13,20],[30,2],[22,0],[23,19],[19,9],[18,5],[2,12],[29,26],[10,7],[30,8],[12,27],[3,10],[14,3],[10,1],[23,14],[7,8],[25,26],[19,10],[0,29],[16,14],[19,12],[14,12],[5,20],[17,21],[6,12],[15,7],[1,13],[21,26],[14,13],[18,29],[0,26],[26,15],[24,19],[23,31],[18,2],[29,15],[28,2],[8,5],[20,22],[14,8],[16,18],[1,24],[13,28],[20,23],[4,22],[28,12],[4,3],[26,28],[5,9],[3,19],[6,26],[10,9],[20,21],[7,23],[28,20],[31,4],[16,19],[6,16],[13,19],[24,27],[17,29],[24,28],[25,8],[23,28],[5,10],[25,26],[27,29],[17,31],[8,0],[1,27],[3,21],[31,18],[27,24],[2,1],[30,16],[22,3],[9,30],[12,10],[30,2],[29,3],[7,13],[9,14],[11,13],[29,13],[26,9],[30,15],[6,18],[29,25],[23,30],[31,23],[14,11],[25,22],[8,25],[24,29],[3,27],[21,22],[12,29],[23,16],[18,14],[30,7],[6,24],[18,22],[10,22],[8,27],[27,0],[10,21],[5,29],[23,2],[30,7],[22,0],[2,24],[1,31],[21,25],[14,7],[5,2],[28,30],[22,24],[16,0],[1,13],[19,29],[30,20],[3,0],[23,28],[0,15],[13,28],[28,10],[7,11],[30,6],[21,7],[18,16],[6,23],[21,6],[28,6],[10,30],[30,25],[6,22],[1,29],[4,30],[1,29],[0,12],[11,12],[3,0],[2,31],[9,17],[16,22],[21,26],[27,9],[5,11],[15,13],[24,21],[1,23],[31,18],[5,11],[31,0],[27,3],[2,22],[9,20],[23,11],[29,24],[21,6],[31,14],[4,12],[16,9],[15,12],[18,28],[29,21],[0,27],[17,10],[15,14],[8,27],[7,20],[6,29],[21,20],[26,0],[8,4],[24,17],[17,27],[13,8],[20,9],[27,17],[7,31],[0,2],[15,7],[8,17],[27,8],[30,5],[20,14],[1,21],[11,31],[15,10],[6,19],[10,5],[11,28],[17,3],[30,22],[5,3],[0,15],[6,17],[10,24],[28,9],[16,0],[11,24],[0,24],[2,7],[21,17],[29,19],[5,15],[0,17],[21,9],[26,29],[4,25],[20,24],[27,31],[9,14],[13,2],[31,27],[26,5],[19,0],[10,21],[18,20],[17,4],[25,21],[22,21],[13,30],[5,23],[11,31],[11,17],[12,9],[8,4],[21,31],[13,7],[25,8],[27,23],[24,5]],[[31,7],[19,0],[12,17],[24,27],[0,14],[4,21],[31,30],[26,5],[14,7],[16,1],[13,12],[24,13],[12,30],[9,0],[12,0],[10,31],[19,4],[13,29],[14,18],[4,13],[24,13],[31,13],[18,14],[9,30],[25,30],[30,18],[26,15],[5,8],[31,24],[7,4],[8,13],[10,9],[8,16],[18,27],[0,3],[12,21],[17,16],[11,27],[27,21],[26,17],[29,26],[17,18],[2,6],[15,20],[4,5],[26,16],[5,16],[28,4],[18,1],[9,1],[3,13],[0,23],[17,6],[6,23],[7,23],[9,8],[12,19],[14,3],[23,3],[31,11],[16,28],[18,5],[3,22],[18,2],[22,4],[1,17],[30,4],[15,20],[26,11],[21,25],[3,30],[19,15],[6,20],[11,20],[8,13],[7,6],[3,11],[25,11],[14,31],[8,5],[15,7],[26,8],[19,25],[23,5],[12,14],[27,4],[7,29],[7,20],[29,28],[9,5],[29,7],[14,27],[27,30],[4,6],[25,15],[23,31],[22,27],[19,17],[29,0],[17,16],[7,28],[26,12],[5,16],[20,16],[31,1],[7,11],[27,21],[21,29],[20,13],[24,8],[15,30],[7,9],[11,24],[26,8],[2,24],[14,6],[17,16],[9,28],[12,24],[23,29],[0,2],[9,10],[25,9],[3,22],[22,31],[4,17],[26,21],[1,2],[6,24],[29,27],[5,12],[8,1],[5,9],[17,19],[0,2],[17,19],[17,28],[26,22],[27,11],[14,31],[27,19],[6,10],[26,23],[22,20],[0,14],[26,3],[10,17],[3,2],[16,5],[15,9],[19,30],[10,5],[15,14],[21,5],[24,18],[26,24],[9,12],[9,20],[21,10],[10,23],[18,24],[23,0],[20,8],[20,8],[19,1],[19,5],[3,7],[10,2],[22,29],[13,11],[8,18],[8,30],[3,7],[29,15],[30,9],[28,15],[1,28],[24,10],[10,19],[0,8],[24,25],[9,26],[11,21],[26,24],[31,11],[30,0],[2,31],[27,19],[25,30],[30,1],[23,12],[1,16],[20,12],[10,31],[7,17],[4,7],[9,6],[16,12],[14,27],[10,9],[15,7],[18,0],[7,4],[29,23],[0,11],[25,18],[17,20],[25,3],[0,29],[5,19],[27,28],[18,15],[10,1],[11,0],[24,23],[15,24],[5,3],[15,24],[9,24],[4,31],[27,24],[30,5],[0,9],[28,0],[23,17],[17,26],[29,20],[31,22],[11,6],[18,16],[13,16],[0,10],[20,29],[1,23],[28,1],[16,28],[31,22],[11,14],[2,0],[27,16],[3,26],[11,20],[23,20],[21,28],[5,8],[2,5],[1,15],[5,22],[24,20],[8,30],[30,17],[5,24],[6,3],[24,9],[19,5],[24,27]],[[9,1],[18,0],[10,18],[1,18],[5,24],[22,17],[10,26],[4,16],[28,1],[2,9],[23,7],[6,30],[2,27],[30,16],[10,19],[6,1],[10,7],[24,17],[2,23],[17,13],[23,12],[25,16],[5,30],[26,0],[27,28],[12,25],[27,23],[13,2],[0,4],[7,16],[26,22],[17,0],[8,20],[8,30],[17,4],[10,7],[11,2],[9,21],[10,25],[5,0],[24,6],[13,26],[5,20],[11,5],[18,2],[7,23],[24,9],[10,29],[23,20],[15,22],[17,15],[3,21],[26,8],[28,1],[21,5],[21,23],[16,19],[28,17],[13,31],[16,21],[19,26],[2,29],[11,15],[10,28],[8,10],[5,25],[19,3],[27,26],[3,2],[9,26],[8,3],[5,30],[6,3],[22,31],[16,27],[2,21],[7,16],[2,18],[14,28],[31,11],[11,3],[23,1],[24,1],[23,30],[19,28],[10,5],[4,15],[7,29],[11,0],[23,14],[30,1],[11,28],[26,31],[21,19],[2,26],[17,21],[27,29],[29,11],[6,21],[2,23],[25,16],[31,19],[23,7],[11,10],[6,18],[23,7],[25,6],[6,28],[23,31],[10,21],[21,12],[26,1],[14,0],[13,24],[10,30],[5,8],[27,19],[20,24],[18,17],[3,0],[5,7],[30,4],[0,21],[9,31],[8,4],[18,26],[0,17],[0,5],[10,17],[23,6],[17,8],[12,7],[26,11],[28,13],[1,10],[25,7],[0,31],[4,24],[3,22],[15,19],[26,27],[9,14],[14,6],[21,8],[17,15],[13,10],[12,20],[27,0],[8,9],[14,15],[14,5],[3,5],[1,27],[5,21],[2,10],[13,24],[31,16],[6,17],[12,5],[11,19],[31,16],[11,15],[22,6],[12,28],[18,17],[14,22],[4,11],[18,27],[23,27],[30,0],[10,21],[2,31],[5,28],[1,17],[6,28],[26,2],[11,0],[10,12],[4,24],[7,12],[20,29],[21,31],[24,2],[7,3],[7,11],[20,18],[13,29],[24,4],[23,9],[31,7],[11,13],[5,24],[0,29],[1,20],[27,22],[17,2],[31,15],[1,2],[12,5],[19,17],[14,2],[21,11],[12,6],[5,1],[27,6],[25,0],[5,3],[9,29],[3,7],[25,17],[31,8],[0,4],[29,5],[30,1],[22,24],[9,12],[5,0],[16,25],[19,22],[20,18],[20,27],[14,21],[16,26],[10,28],[18,2],[10,3],[27,1],[9,1],[0,5],[19,18],[30,6],[6,2],[0,11],[30,5],[9,1],[24,10],[22,9],[8,17],[10,28],[9,14],[31,18],[15,6],[27,25],[13,2],[6,9],[6,14],[20,23],[6,16],[23,31],[16,5],[18,17],[16,21],[0,29],[23,1],[14,29],[13,17]],[[1,17],[31,17],[3,23],[15,16],[20,4],[21,31],[27,24],[5,24],[4,3],[30,9],[6,15],[12,26],[12,28],[16,4],[17,15],[9,17],[27,15],[5,31],[3,28],[21,25],[16,7],[15,6],[31,24],[11,13],[0,1],[2,27],[15,16],[21,31],[18,30],[11,14],[16,6],[31,28],[6,4],[5,3],[31,30],[3,14],[27,14],[29,24],[15,16],[8,15],[8,26],[10,16],[29,16],[15,10],[29,22],[4,21],[4,26],[13,20],[16,22],[13,2],[0,16],[28,2],[28,8],[1,16],[19,28],[3,11],[13,28],[21,25],[18,20],[3,4],[4,15],[12,10],[28,5],[25,31],[1,11],[3,15],[27,13],[15,23],[5,22],[4,0],[18,26],[10,28],[28,3],[27,28],[19,31],[22,12],[5,4],[6,22],[9,26],[0,19],[8,24],[5,7],[19,7],[10,20],[12,20],[28,20],[2,18],[9,0],[2,29],[25,28],[25,9],[15,11],[31,26],[28,13],[13,2],[20,22],[16,12],[9,21],[11,2],[11,25],[0,30],[16,25],[8,29],[26,5],[10,31],[31,11],[20,23],[7,13],[9,14],[19,20],[6,15],[20,19],[10,4],[25,14],[29,17],[5,20],[14,27],[24,8],[12,0],[13,12],[9,2],[29,28],[17,27],[0,23],[21,5],[6,18],[5,18],[13,25],[28,29],[10,16],[4,17],[31,22],[0,26],[9,20],[19,24],[18,25],[9,8],[21,16],[24,27],[30,26],[11,0],[5,6],[10,15],[30,8],[15,0],[8,15],[10,22],[25,13],[25,24],[7,9],[13,30],[1,9],[27,20],[9,30],[24,27],[29,21],[6,4],[9,27],[6,16],[17,26],[29,15],[5,21],[14,30],[21,27],[15,20],[29,11],[28,29],[21,8],[10,22],[24,29],[29,27],[22,5],[11,18],[16,25],[27,20],[2,13],[23,17],[26,29],[16,14],[11,16],[8,27],[28,10],[14,19],[17,12],[10,25],[18,9],[27,29],[14,18],[19,3],[6,28],[16,3],[16,19],[27,26],[31,2],[0,14],[30,17],[23,12],[25,0],[26,22],[26,14],[7,11],[4,29],[0,19],[7,17],[17,20],[31,3],[0,2],[16,28],[0,23],[8,0],[2,28],[13,5],[1,4],[25,8],[9,14],[30,1],[19,14],[24,26],[17,2],[4,31],[5,6],[4,20],[19,13],[5,15],[6,4],[3,25],[29,19],[21,9],[29,28],[14,26],[31,11],[26,1],[24,18],[24,17],[20,23],[13,9],[5,26],[26,15],[4,15],[8,22],[14,7],[27,7],[7,10],[21,27],[4,31],[8,11],[16,30],[7,21],[7,5],[24,30],[2,16],[25,19],[25,14],[23,20],[15,0],[19,13]],[[8,26],[10,13],[18,16],[3,31],[5,25],[9,14],[30,17],[21,18],[7,2],[25,10],[26,0],[3,5],[22,15],[5,26],[21,29],[9,11],[18,4],[28,30],[16,27],[0,19],[17,20],[14,24],[16,2],[14,11],[15,18],[7,11],[3,21],[25,10],[25,14],[19,25],[30,0],[3,29],[29,18],[2,19],[26,6],[1,5],[2,17],[20,7],[17,19],[2,21],[4,11],[8,17],[4,24],[16,3],[9,22],[28,25],[20,8],[3,30],[22,10],[28,8],[24,27],[29,22],[16,18],[18,28],[13,22],[24,17],[4,14],[24,5],[24,30],[31,11],[18,7],[5,19],[17,25],[20,14],[29,30],[27,14],[6,31],[18,17],[7,11],[3,23],[4,3],[19,26],[14,27],[30,6],[6,17],[9,1],[13,25],[16,26],[12,0],[22,27],[24,17],[4,20],[20,3],[24,20],[8,30],[13,0],[5,29],[6,19],[5,27],[31,2],[3,28],[29,28],[27,6],[26,3],[25,27],[9,10],[15,31],[4,20],[1,19],[29,11],[12,5],[19,30],[19,15],[26,19],[22,23],[17,16],[4,24],[2,18],[19,13],[31,20],[5,6],[29,16],[20,9],[8,23],[28,24],[6,13],[9,20],[4,20],[14,9],[26,7],[28,4],[18,25],[22,19],[15,2],[21,0],[10,24],[7,17],[21,4],[8,3],[2,15],[6,30],[24,23],[28,25],[2,25],[29,31],[30,24],[18,16],[29,13],[2,9],[28,9],[31,7],[3,6],[28,30],[12,27],[7,9],[25,2],[18,4],[25,22],[6,8],[9,23],[23,18],[25,0],[18,24],[18,25],[1,15],[15,28],[3,27],[6,16],[16,31],[8,31],[30,19],[4,28],[23,5],[31,7],[5,3],[22,23],[1,16],[2,15],[15,12],[25,23],[8,30],[20,9],[28,15],[12,15],[4,21],[20,4],[7,9],[14,9],[10,21],[24,15],[17,24],[5,26],[16,24],[28,20],[15,24],[16,23],[7,29],[7,22],[2,30],[12,9],[4,20],[28,13],[19,12],[28,8],[13,24],[30,24],[10,27],[9,4],[17,18],[29,12],[30,4],[18,12],[25,0],[19,9],[20,13],[8,15],[29,14],[21,30],[20,31],[16,6],[27,0],[13,24],[19,7],[12,8],[1,9],[20,2],[26,30],[29,2],[1,0],[25,30],[10,1],[12,30],[3,10],[9,27],[3,1],[17,12],[18,20],[19,8],[21,18],[15,28],[19,12],[25,16],[23,4],[1,12],[19,2],[14,22],[26,6],[13,17],[4,24],[28,25],[7,29],[21,15],[30,23],[25,21],[10,19],[4,20],[26,0],[31,22],[13,29],[4,0],[4,19],[13,21],[26,17],[3,29],[0,11],[6,29]],[[19,20],[11,13],[1,15],[23,28],[14,12],[29,2],[30,27],[0,20],[9,30],[1,25],[11,10],[6,23],[10,25],[6,10],[3,26],[18,14],[22,27],[9,22],[9,14],[7,4],[2,13],[30,3],[6,31],[30,24],[23,30],[3,4],[6,21],[10,7],[31,26],[19,6],[25,28],[20,5],[30,6],[0,8],[14,0],[13,23],[3,24],[2,26],[11,10],[30,11],[8,30],[6,10],[25,5],[9,6],[2,17],[12,13],[22,18],[2,30],[22,5],[27,14],[10,29],[6,20],[25,19],[13,15],[5,14],[19,13],[13,4],[22,30],[24,20],[0,31],[6,25],[27,29],[24,8],[21,14],[12,10],[22,15],[1,2],[4,1],[6,25],[10,8],[26,31],[27,25],[0,29],[16,2],[9,13],[7,17],[23,4],[27,14],[29,17],[26,20],[26,22],[1,28],[11,25],[25,11],[20,6],[25,26],[8,5],[5,29],[26,12],[14,29],[12,3],[24,29],[20,28],[22,10],[9,11],[9,6],[6,10],[6,14],[28,6],[1,22],[25,10],[21,27],[12,26],[15,28],[9,0],[9,27],[26,27],[26,12],[11,1],[28,4],[16,10],[12,25],[23,1],[31,27],[11,22],[0,25],[22,13],[23,30],[7,11],[2,31],[14,6],[31,4],[25,19],[13,11],[8,22],[27,28],[19,26],[29,10],[17,12],[6,22],[3,26],[31,30],[24,25],[30,4],[18,0],[6,21],[25,30],[24,23],[16,26],[8,6],[3,15],[10,22],[17,31],[25,24],[1,6],[27,17],[23,31],[1,22],[11,7],[31,6],[26,5],[10,20],[22,18],[8,0],[17,29],[3,24],[30,5],[2,17],[15,27],[6,12],[25,28],[2,6],[8,2],[26,29],[1,3],[0,21],[21,0],[30,5],[7,8],[25,21],[21,19],[19,10],[19,1],[16,12],[30,29],[19,25],[4,7],[24,30],[29,6],[24,8],[6,2],[7,23],[17,18],[18,0],[6,31],[24,8],[27,22],[0,10],[7,22],[20,8],[11,17],[22,10],[13,10],[1,2],[14,16],[16,25],[5,29],[16,6],[21,16],[18,23],[3,5],[12,23],[19,29],[31,14],[2,19],[29,1],[26,1],[10,23],[29,23],[24,30],[15,27],[23,26],[15,7],[7,3],[31,18],[4,20],[28,10],[13,28],[14,21],[25,15],[28,0],[24,23],[8,12],[26,18],[11,2],[23,11],[16,0],[27,21],[18,27],[10,9],[17,15],[27,13],[28,16],[21,19],[14,0],[6,12],[10,12],[29,16],[15,29],[27,23],[3,23],[10,15],[16,24],[23,17],[13,25],[12,22],[28,10],[14,4],[20,10],[9,31],[19,17],[25,1],[18,6],[20,13],[27,21],[18,28]]]
YW = 551
def setup_inputs(rng):
    return {"x": rng.standard_normal((N, 128, T), dtype=np.float32)}
def reference(x):
    y = np.full((N, 128, YW), np.nan, x.dtype)
    fill = [0] * N
    for r in range(N):
        for t in range(T):
            for e in ROUTE[r][t]:
                y[e][:, fill[e]] = x[r][:, t]
                fill[e] += 1
    return {"y": y}

@@ -1,0 +1,227 @@
+from concourse.bass import DstId, RemoteDMATransfer
+
+NSLOT = 6
+PACKW = 112
+RC = 2
+SAME = (0, 1, 4, 5)
+OTHER = (2, 3, 6, 7)
+FULL = tuple(1 << i for i in range(16))
+TRIM = (0x0F00, 0xF000, 0x00FF)
+XCALLS = (FULL, FULL, TRIM)
+ADJ = (0, 0, 0, 0, 0, 0, 0, 0)
+SHARE_ORDER = (3, 0, 1, 6, 7, 4, 5)
+AHEAD = 0
+GPAIRS = 0
+
+SCRATCH = {
+    "xs": ("sbuf", [128, 256], "float32"),
+    "pack": ("sbuf", [128, PACKW], "float32"),
+    "land": ("sbuf", [128, 551], "float32"),
+}
+SEMAPHORES = ["ld", "xa", "sent", "arr", "st", "gg"] + ["gh%d" % s for s in range(NSLOT)]
+
+CACHE = {}
+
+
+def bits(m):
+    return bin(m).count("1")
+
+
+def tables(tabs):
+    if "cnt" not in CACHE:
+        route = tabs["ROUTE"]
+        n = len(route)
+        cnt = [[0] * n for _ in range(n)]
+        for r in range(n):
+            for es in route[r]:
+                for e in es:
+                    cnt[r][e] += 1
+        off = [[0] * n for _ in range(n)]
+        for e in range(n):
+            a = 0
+            for r in range(n):
+                off[r][e] = a
+                a += cnt[r][e]
+        CACHE["cnt"], CACHE["off"] = cnt, off
+    return CACHE["cnt"], CACHE["off"]
+
+
+def chip_plan(r, tabs):
+    key = ("plan", r)
+    if key in CACHE:
+        return CACHE[key]
+    route = tabs["ROUTE"]
+    n = len(route)
+    cnt, off = tables(tabs)
+    toks = [[] for _ in range(n)]
+    for t, es in enumerate(route[r]):
+        for e in es:
+            toks[e].append(t)
+    runs = []
+    for e in range(n):
+        rs = []
+        for i, t in enumerate(toks[e]):
+            if rs and rs[-1][0] + rs[-1][1] == t:
+                rs[-1] = (rs[-1][0], rs[-1][1] + 1, rs[-1][2])
+            else:
+                rs.append((t, 1, i))
+        runs.append(rs)
+    own = [[] for _ in range(8)]
+    load = [0] * 8
+    load[RC] += len(runs[r])
+    for group, par in ((SAME, 0), (OTHER, 1)):
+        ds = [e for e in range(n) if e != r and (e + r) % 2 == par and toks[e]]
+        for e in sorted(ds, key=lambda e: (-len(runs[e]), e)):
+            k = min(group, key=lambda k: (load[k], k))
+            own[k].append(e)
+            load[k] += len(runs[e])
+    cores = []
+    for k in range(8):
+        own[k].sort(key=lambda e: (e - r) % n)
+        slots, units, base = [], [], 0
+        for e in own[k]:
+            s = len(slots)
+            slots.append((e, "pack", base, len(toks[e])))
+            units += [(s, t0, ln, "pack", base + i) for (t0, ln, i) in runs[e]]
+            base += len(toks[e])
+        if k == RC and toks[r]:
+            s = len(slots)
+            slots.append((r, "land", off[r][r], len(toks[r])))
+            units += [(s, t0, ln, "land", off[r][r] + i) for (t0, ln, i) in runs[r]]
+        assert base <= PACKW and len(slots) <= NSLOT
+        cores.append({"slots": slots, "units": units, "xcalls": [], "local": [], "pairs": [], "tot": [0] * len(slots)})
+    total = sum(len(c["units"]) for c in cores)
+    keep_all = total - 8 * sum(len(p) for p in XCALLS)
+    keep = [keep_all // 8 + ADJ[k] for k in range(8)]
+    k = 0
+    while sum(keep) < keep_all:
+        keep[k % 8] += 1
+        k += 1
+    pool = []
+    for k in range(8):
+        us = cores[k]["units"]
+        give = max(0, len(us) - keep[k])
+        i = 0
+        for u in us:
+            if u[2] == 1 and i < give:
+                pool.append((i, k, u))
+                i += 1
+            else:
+                cores[k]["local"].append(u)
+    pool.sort(key=lambda p: (p[0], p[1]))
+    for ci, pat in enumerate(XCALLS):
+        for k in range(8):
+            x = (k + ci) % 8
+            call = []
+            for m in pat:
+                j = 0
+                while j < len(pool) and pool[j][1] == x:
+                    j += 1
+                if j == len(pool):
+                    break
+                (_, o, (s, t0, ln, buf, col)) = pool.pop(j)
+                call.append((m, t0, o, buf, col, s))
+                cores[o]["tot"][s] += bits(m)
+            if call:
+                cores[x]["xcalls"].append(call)
+    for (_, o, u) in pool:
+        cores[o]["local"].append(u)
+    for c in cores:
+        c["local"].sort(key=lambda u: (u[0], u[4]))
+        i = len(c["local"]) - 1
+        while i > 0 and len(c["pairs"]) < GPAIRS:
+            a, b = c["local"][i - 1], c["local"][i]
+            if a[0] == b[0] and a[2] == 1 and b[2] == 1:
+                c["pairs"].append((a, b))
+                del c["local"][i - 1:i + 1]
+                i -= 2
+            else:
+                i -= 1
+        for u in c["local"]:
+            c["tot"][u[0]] += 16
+    CACHE[key] = cores
+    return cores
+
+
+def rank_program(g, core, T, topo):
+    k = core % 8
+    base = core - k
+    r = T.rank_of(base + RC)
+    tabs = T.tables
+    cnt, off = tables(tabs)
+    n = len(cnt)
+    me = chip_plan(r, tabs)[k]
+    S = T.sem
+    sent = 0
+
+    if k == RC:
+        g.sync.dma_start(T.xs[:], T.x[:]).then_inc(S.ld, 16)
+        ready = S.ld
+        g.wait_ge(ready, 16)
+        ids = []
+        for h in SHARE_ORDER:
+            rid, pid = topo.addr(base + h, core)
+            ids.append(DstId(rid=rid, pnc=pid))
+        g.remote_dma_fused([RemoteDMATransfer(dst_ids=ids, dma_engine_mask=0xFFFF, remote_sem=S.xa,
+                                              srcs=[T.xs[:]], dsts=[T.xs[:] for _ in ids])], local_sem=S.sent)
+        sent += 16
+    else:
+        ready = S.xa
+        g.wait_ge(ready, 16)
+    g.sync.wait_ge(ready, 16)
+    g.scalar.wait_ge(ready, 16)
+
+    for call in me["xcalls"]:
+        trs = []
+        for (m, t, o, buf, col, s) in call:
+            rid, pid = topo.addr(base + o, core)
+            trs.append(RemoteDMATransfer(dst_ids=[DstId(rid=rid, pnc=pid)], dma_engine_mask=m,
+                                         remote_sem=S["gh%d" % s], src=T.xs[:, t:t + 1], dst=T[buf][:, col:col + 1]))
+            sent += bits(m)
+        g.remote_dma_fused(trs, local_sem=S.sent)
+
+    qs = (g.sync, g.scalar)
+    gate = [-1, -1]
+    for i, (s, t0, ln, buf, col) in enumerate(me["local"]):
+        q = i % 2
+        if AHEAD and s - AHEAD > gate[q]:
+            gate[q] = s - AHEAD
+            if me["tot"][gate[q]]:
+                qs[q].wait_ge(S["gh%d" % gate[q]], me["tot"][gate[q]])
+        qs[q].dma_start(T[buf][:, col:col + ln], T.xs[:, t0:t0 + ln]).then_inc(S["gh%d" % s], 16)
+    gslots = set()
+    for (a, b) in me["pairs"]:
+        dt_, dc = b[1] - a[1], b[4] - a[4]
+        g.dma_start(T[a[3]][:, a[4]:b[4] + 1:dc], T.xs[:, a[1]:b[1] + 1:dt_],
+                    allow_slow_non_contiguous=True).then_inc(S.gg, 16)
+        gslots.add(a[0])
+
+    gwait = False
+    for s, (e, buf, b, w) in enumerate(me["slots"]):
+        if e == r:
+            continue
+        if me["tot"][s]:
+            g.wait_ge(S["gh%d" % s], me["tot"][s])
+        if s in gslots and not gwait:
+            g.wait_ge(S.gg, 16 * len(me["pairs"]))
+            gwait = True
+        dst = T.cores[e]
+        rid, pid = topo.addr(dst, core)
+        m = topo.mask(core, dst)
+        g.remote_dma(T.land[:, off[r][e]:off[r][e] + w], T.pack[:, b:b + w], S.arr, S.sent, pid, rid, m)
+        sent += bits(m)
+    if me["pairs"] and not gwait:
+        g.wait_ge(S.gg, 16 * len(me["pairs"]))
+    g.wait_ge(S.sent, sent)
+
+    if k == RC:
+        g.sync.wait_ge(S.arr, 8 * sum(1 for q in range(n) if q != r and cnt[q][r]))
+        for s, (e, buf, b, w) in enumerate(me["slots"]):
+            if e == r:
+                if me["tot"][s]:
+                    g.sync.wait_ge(S["gh%d" % s], me["tot"][s])
+                if s in gslots:
+                    g.sync.wait_ge(S.gg, 16 * len(me["pairs"]))
+        width = sum(cnt[q][r] for q in range(n))
+        g.sync.dma_start(T.y[:, 0:width], T.land[:, 0:width]).then_inc(S.st, 16)
+        g.sync.wait_ge(S.st, 16)

@@ -5,20 +5,19 @@ PACKW = 112
 RC = 2
 SAME = (0, 1, 4, 5)
 OTHER = (2, 3, 6, 7)
-FULL = tuple(1 << i for i in range(16))
-TRIM = (0x0F00, 0xF000, 0x00FF)
-XCALLS = (FULL, FULL, TRIM)
-ADJ = (0, 0, 0, 0, 0, 0, 0, 0)
-SHARE_ORDER = (3, 0, 1, 6, 7, 4, 5)
+LO, HI, ALL = (0, 128), (128, 256), (0, 256)
+HOLD = (LO, HI, ALL, HI, LO, HI, LO, HI)
+RHOME = LO
+XROOM = 36
+LADJ = (0, 0, 0, 0, 0, 0, 0, 0)
 AHEAD = 0
-GPAIRS = 0
 
 SCRATCH = {
     "xs": ("sbuf", [128, 256], "float32"),
     "pack": ("sbuf", [128, PACKW], "float32"),
     "land": ("sbuf", [128, 551], "float32"),
 }
-SEMAPHORES = ["ld", "xa", "sent", "arr", "st", "gg"] + ["gh%d" % s for s in range(NSLOT)]
+SEMAPHORES = ["ld", "xa", "sent", "arr", "st"] + ["gh%d" % s for s in range(NSLOT)]
 
 CACHE = {}
 
@@ -46,6 +45,62 @@ def tables(tabs):
     return CACHE["cnt"], CACHE["off"]
 
 
+def ports(r, e, d):
+    if (r + e) % 2 == 0:
+        return (("out", r, d), ("in", e, d))
+    if e == r ^ 1:
+        return (("mate", r, d),)
+    return (("mate", r, d), ("out", r ^ 1, d), ("in", e, d))
+
+
+def dies(tabs):
+    if "die" in CACHE:
+        return CACHE["die"]
+    cnt, off = tables(tabs)
+    n = len(cnt)
+    die, load = {}, {}
+    for r in range(n):
+        for e in range(n):
+            if e != r:
+                die[(r, e)] = (((e - r) % n) // 2) % 2
+                for p in ports(r, e, die[(r, e)]):
+                    load[p] = load.get(p, 0) + cnt[r][e]
+    for sweep in range(8):
+        changed = 0
+        for r in range(n):
+            for par in (0, 1):
+                ds = [e for e in range(n) if e != r and (e + r) % 2 == par]
+                for a in ds:
+                    for b in ds:
+                        if die[(r, a)] == 0 and die[(r, b)] == 1:
+                            diff = {}
+                            for (e, nd) in ((a, 1), (b, 0)):
+                                for p in ports(r, e, 1 - nd):
+                                    diff[p] = diff.get(p, 0) - cnt[r][e]
+                                for p in ports(r, e, nd):
+                                    diff[p] = diff.get(p, 0) + cnt[r][e]
+                            if sum((load.get(p, 0) + v) ** 2 - load.get(p, 0) ** 2 for p, v in diff.items()) < 0:
+                                for p, v in diff.items():
+                                    load[p] = load.get(p, 0) + v
+                                die[(r, a)], die[(r, b)] = 1, 0
+                                changed += 1
+        if not changed:
+            break
+    CACHE["die"] = die
+    return die
+
+
+def holds(k, t0, ln):
+    return HOLD[k][0] <= t0 and t0 + ln <= HOLD[k][1]
+
+
+def masks(m):
+    w = 1
+    while m * w * 2 <= 16:
+        w *= 2
+    return [((1 << w) - 1) << (16 - w * (i + 1)) for i in range(m)]
+
+
 def chip_plan(r, tabs):
     key = ("plan", r)
     if key in CACHE:
@@ -66,13 +121,15 @@ def chip_plan(r, tabs):
             else:
                 rs.append((t, 1, i))
         runs.append(rs)
+    die = dies(tabs)
     own = [[] for _ in range(8)]
     load = [0] * 8
     load[RC] += len(runs[r])
     for group, par in ((SAME, 0), (OTHER, 1)):
         ds = [e for e in range(n) if e != r and (e + r) % 2 == par and toks[e]]
         for e in sorted(ds, key=lambda e: (-len(runs[e]), e)):
-            k = min(group, key=lambda k: (load[k], k))
+            pair = group[0:2] if die[(r, e)] == 1 else group[2:4]
+            k = min(pair, key=lambda k: (load[k], k))
             own[k].append(e)
             load[k] += len(runs[e])
     cores = []
@@ -89,54 +146,54 @@ def chip_plan(r, tabs):
             slots.append((r, "land", off[r][r], len(toks[r])))
             units += [(s, t0, ln, "land", off[r][r] + i) for (t0, ln, i) in runs[r]]
         assert base <= PACKW and len(slots) <= NSLOT
-        cores.append({"slots": slots, "units": units, "xcalls": [], "local": [], "pairs": [], "tot": [0] * len(slots)})
-    total = sum(len(c["units"]) for c in cores)
-    keep_all = total - 8 * sum(len(p) for p in XCALLS)
-    keep = [keep_all // 8 + ADJ[k] for k in range(8)]
-    k = 0
-    while sum(keep) < keep_all:
-        keep[k % 8] += 1
-        k += 1
-    pool = []
+        cores.append({"slots": slots, "units": units, "xlist": [], "xcalls": [], "local": [], "tot": [0] * len(slots)})
+    room = [XROOM] * 8
+    left = []
+
+    def space(o, t):
+        return max(room[k] for k in range(8) if k != o and holds(k, t, 1))
+
+    def hand(o, u):
+        x = max((k for k in range(8) if k != o and holds(k, u[1], 1)),
+                key=lambda k: (room[k] > 0 and (k != RC or RHOME[0] <= u[1] < RHOME[1]), room[k], -k))
+        room[x] -= 1
+        cores[x]["xlist"].append((o, u))
+
     for k in range(8):
-        us = cores[k]["units"]
-        give = max(0, len(us) - keep[k])
-        i = 0
-        for u in us:
-            if u[2] == 1 and i < give:
-                pool.append((i, k, u))
-                i += 1
-            else:
-                cores[k]["local"].append(u)
-    pool.sort(key=lambda p: (p[0], p[1]))
-    for ci, pat in enumerate(XCALLS):
+        left.append([u for u in cores[k]["units"] if holds(k, u[1], u[2])])
+    for i in range(max(len(c["units"]) for c in cores)):
         for k in range(8):
-            x = (k + ci) % 8
-            call = []
-            for m in pat:
-                j = 0
-                while j < len(pool) and pool[j][1] == x:
-                    j += 1
-                if j == len(pool):
+            us = cores[k]["units"]
+            if i < len(us) and not holds(k, us[i][1], us[i][2]):
+                for j in range(us[i][2]):
+                    hand(k, (us[i][0], us[i][1] + j, 1, us[i][3], us[i][4] + j))
+    while True:
+        best = None
+        for o in sorted(range(8), key=lambda k: (-len(left[k]) + LADJ[k], k)):
+            ones = [u for u in left[o] if u[2] == 1]
+            if ones:
+                u = max(ones, key=lambda u: (space(o, u[1]), -u[0], -u[4]))
+                if space(o, u[1]) > 0:
+                    best = (o, u)
                     break
-                (_, o, (s, t0, ln, buf, col)) = pool.pop(j)
+        if not best:
+            break
+        left[best[0]].remove(best[1])
+        hand(best[0], best[1])
+    for k in range(8):
+        cores[k]["local"] = left[k]
+        cores[k]["xlist"].sort(key=lambda p: (p[1][0], p[0]))
+    for c in cores:
+        xl = c["xlist"]
+        for a in range(0, len(xl), 16):
+            part = xl[a:a + 16]
+            call = []
+            for m, (o, (s, t0, ln, buf, col)) in zip(masks(len(part)), part):
                 call.append((m, t0, o, buf, col, s))
                 cores[o]["tot"][s] += bits(m)
-            if call:
-                cores[x]["xcalls"].append(call)
-    for (_, o, u) in pool:
-        cores[o]["local"].append(u)
+            c["xcalls"].append(call)
     for c in cores:
         c["local"].sort(key=lambda u: (u[0], u[4]))
-        i = len(c["local"]) - 1
-        while i > 0 and len(c["pairs"]) < GPAIRS:
-            a, b = c["local"][i - 1], c["local"][i]
-            if a[0] == b[0] and a[2] == 1 and b[2] == 1:
-                c["pairs"].append((a, b))
-                del c["local"][i - 1:i + 1]
-                i -= 2
-            else:
-                i -= 1
         for u in c["local"]:
             c["tot"][u[0]] += 16
     CACHE[key] = cores
@@ -154,22 +211,28 @@ def rank_program(g, core, T, topo):
     S = T.sem
     sent = 0
 
+    parts = sorted(set(HOLD[h] for h in range(8) if h != RC))
+    eng = 16 // len(parts)
     if k == RC:
         g.sync.dma_start(T.xs[:], T.x[:]).then_inc(S.ld, 16)
-        ready = S.ld
-        g.wait_ge(ready, 16)
-        ids = []
-        for h in SHARE_ORDER:
-            rid, pid = topo.addr(base + h, core)
-            ids.append(DstId(rid=rid, pnc=pid))
-        g.remote_dma_fused([RemoteDMATransfer(dst_ids=ids, dma_engine_mask=0xFFFF, remote_sem=S.xa,
-                                              srcs=[T.xs[:]], dsts=[T.xs[:] for _ in ids])], local_sem=S.sent)
-        sent += 16
+        ready, rval = S.ld, 16
+        g.wait_ge(ready, rval)
+        trs = []
+        for i, (a, b) in enumerate(parts):
+            ids = []
+            for h in range(8):
+                if h != RC and HOLD[h] == (a, b):
+                    rid, pid = topo.addr(base + h, core)
+                    ids.append(DstId(rid=rid, pnc=pid))
+            trs.append(RemoteDMATransfer(dst_ids=ids, dma_engine_mask=((1 << eng) - 1) << (eng * i), remote_sem=S.xa,
+                                         srcs=[T.xs[:, a:b]], dsts=[T.xs[:, a:b] for _ in ids]))
+            sent += eng
+        g.remote_dma_fused(trs, local_sem=S.sent)
     else:
-        ready = S.xa
-        g.wait_ge(ready, 16)
-    g.sync.wait_ge(ready, 16)
-    g.scalar.wait_ge(ready, 16)
+        ready, rval = S.xa, eng
+        g.wait_ge(ready, rval)
+    g.sync.wait_ge(ready, rval)
+    g.scalar.wait_ge(ready, rval)
 
     for call in me["xcalls"]:
         trs = []
@@ -189,39 +252,23 @@ def rank_program(g, core, T, topo):
             if me["tot"][gate[q]]:
                 qs[q].wait_ge(S["gh%d" % gate[q]], me["tot"][gate[q]])
         qs[q].dma_start(T[buf][:, col:col + ln], T.xs[:, t0:t0 + ln]).then_inc(S["gh%d" % s], 16)
-    gslots = set()
-    for (a, b) in me["pairs"]:
-        dt_, dc = b[1] - a[1], b[4] - a[4]
-        g.dma_start(T[a[3]][:, a[4]:b[4] + 1:dc], T.xs[:, a[1]:b[1] + 1:dt_],
-                    allow_slow_non_contiguous=True).then_inc(S.gg, 16)
-        gslots.add(a[0])
 
-    gwait = False
     for s, (e, buf, b, w) in enumerate(me["slots"]):
         if e == r:
             continue
-        if me["tot"][s]:
-            g.wait_ge(S["gh%d" % s], me["tot"][s])
-        if s in gslots and not gwait:
-            g.wait_ge(S.gg, 16 * len(me["pairs"]))
-            gwait = True
+        g.wait_ge(S["gh%d" % s], me["tot"][s])
         dst = T.cores[e]
         rid, pid = topo.addr(dst, core)
         m = topo.mask(core, dst)
         g.remote_dma(T.land[:, off[r][e]:off[r][e] + w], T.pack[:, b:b + w], S.arr, S.sent, pid, rid, m)
         sent += bits(m)
-    if me["pairs"] and not gwait:
-        g.wait_ge(S.gg, 16 * len(me["pairs"]))
     g.wait_ge(S.sent, sent)
 
     if k == RC:
         g.sync.wait_ge(S.arr, 8 * sum(1 for q in range(n) if q != r and cnt[q][r]))
         for s, (e, buf, b, w) in enumerate(me["slots"]):
             if e == r:
-                if me["tot"][s]:
-                    g.sync.wait_ge(S["gh%d" % s], me["tot"][s])
-                if s in gslots:
-                    g.sync.wait_ge(S.gg, 16 * len(me["pairs"]))
+                g.sync.wait_ge(S["gh%d" % s], me["tot"][s])
         width = sum(cnt[q][r] for q in range(n))
         g.sync.dma_start(T.y[:, 0:width], T.land[:, 0:width]).then_inc(S.st, 16)
         g.sync.wait_ge(S.st, 16)

@@ -8,9 +8,8 @@ OTHER = (2, 3, 6, 7)
 LO, HI, ALL = (0, 128), (128, 256), (0, 256)
 HOLD = (LO, HI, ALL, HI, LO, HI, LO, HI)
 RHOME = LO
-XROOM = 36
-LADJ = (0, 0, 0, 0, 0, 0, 0, 0)
-AHEAD = 0
+XROOM = (40, 40, 36, 40, 40, 40, 40, 40)
+LADJ = (3, 3, -6, 1, 1, -1, -1, -3)
 
 SCRATCH = {
     "xs": ("sbuf", [128, 256], "float32"),
@@ -147,7 +146,7 @@ def chip_plan(r, tabs):
             units += [(s, t0, ln, "land", off[r][r] + i) for (t0, ln, i) in runs[r]]
         assert base <= PACKW and len(slots) <= NSLOT
         cores.append({"slots": slots, "units": units, "xlist": [], "xcalls": [], "local": [], "tot": [0] * len(slots)})
-    room = [XROOM] * 8
+    room = list(XROOM)
     left = []
 
     def space(o, t):
@@ -244,14 +243,8 @@ def rank_program(g, core, T, topo):
         g.remote_dma_fused(trs, local_sem=S.sent)
 
     qs = (g.sync, g.scalar)
-    gate = [-1, -1]
     for i, (s, t0, ln, buf, col) in enumerate(me["local"]):
-        q = i % 2
-        if AHEAD and s - AHEAD > gate[q]:
-            gate[q] = s - AHEAD
-            if me["tot"][gate[q]]:
-                qs[q].wait_ge(S["gh%d" % gate[q]], me["tot"][gate[q]])
-        qs[q].dma_start(T[buf][:, col:col + ln], T.xs[:, t0:t0 + ln]).then_inc(S["gh%d" % s], 16)
+        qs[i % 2].dma_start(T[buf][:, col:col + ln], T.xs[:, t0:t0 + ln]).then_inc(S["gh%d" % s], 16)
 
     for s, (e, buf, b, w) in enumerate(me["slots"]):
         if e == r:

from concourse.bass import DstId, RemoteDMATransfer

NSLOT = 6
PACKW = 112
RC = 2
SAME = (0, 1, 4, 5)
OTHER = (2, 3, 6, 7)
LO, HI, ALL = (0, 128), (128, 256), (0, 256)
HOLD = (LO, HI, ALL, HI, LO, HI, LO, HI)
RHOME = LO
XROOM = (40, 40, 36, 40, 40, 40, 40, 40)
LADJ = (3, 3, -6, 1, 1, -1, -1, -3)

SCRATCH = {
    "xs": ("sbuf", [128, 256], "float32"),
    "pack": ("sbuf", [128, PACKW], "float32"),
    "land": ("sbuf", [128, 551], "float32"),
}
SEMAPHORES = ["ld", "xa", "sent", "arr", "st"] + ["gh%d" % s for s in range(NSLOT)]

CACHE = {}


def bits(m):
    return bin(m).count("1")


def tables(tabs):
    if "cnt" not in CACHE:
        route = tabs["ROUTE"]
        n = len(route)
        cnt = [[0] * n for _ in range(n)]
        for r in range(n):
            for es in route[r]:
                for e in es:
                    cnt[r][e] += 1
        off = [[0] * n for _ in range(n)]
        for e in range(n):
            a = 0
            for r in range(n):
                off[r][e] = a
                a += cnt[r][e]
        CACHE["cnt"], CACHE["off"] = cnt, off
    return CACHE["cnt"], CACHE["off"]


def ports(r, e, d):
    if (r + e) % 2 == 0:
        return (("out", r, d), ("in", e, d))
    if e == r ^ 1:
        return (("mate", r, d),)
    return (("mate", r, d), ("out", r ^ 1, d), ("in", e, d))


def dies(tabs):
    if "die" in CACHE:
        return CACHE["die"]
    cnt, off = tables(tabs)
    n = len(cnt)
    die, load = {}, {}
    for r in range(n):
        for e in range(n):
            if e != r:
                die[(r, e)] = (((e - r) % n) // 2) % 2
                for p in ports(r, e, die[(r, e)]):
                    load[p] = load.get(p, 0) + cnt[r][e]
    for sweep in range(8):
        changed = 0
        for r in range(n):
            for par in (0, 1):
                ds = [e for e in range(n) if e != r and (e + r) % 2 == par]
                for a in ds:
                    for b in ds:
                        if die[(r, a)] == 0 and die[(r, b)] == 1:
                            diff = {}
                            for (e, nd) in ((a, 1), (b, 0)):
                                for p in ports(r, e, 1 - nd):
                                    diff[p] = diff.get(p, 0) - cnt[r][e]
                                for p in ports(r, e, nd):
                                    diff[p] = diff.get(p, 0) + cnt[r][e]
                            if sum((load.get(p, 0) + v) ** 2 - load.get(p, 0) ** 2 for p, v in diff.items()) < 0:
                                for p, v in diff.items():
                                    load[p] = load.get(p, 0) + v
                                die[(r, a)], die[(r, b)] = 1, 0
                                changed += 1
        if not changed:
            break
    CACHE["die"] = die
    return die


def holds(k, t0, ln):
    return HOLD[k][0] <= t0 and t0 + ln <= HOLD[k][1]


def masks(m):
    w = 1
    while m * w * 2 <= 16:
        w *= 2
    return [((1 << w) - 1) << (16 - w * (i + 1)) for i in range(m)]


def chip_plan(r, tabs):
    key = ("plan", r)
    if key in CACHE:
        return CACHE[key]
    route = tabs["ROUTE"]
    n = len(route)
    cnt, off = tables(tabs)
    toks = [[] for _ in range(n)]
    for t, es in enumerate(route[r]):
        for e in es:
            toks[e].append(t)
    runs = []
    for e in range(n):
        rs = []
        for i, t in enumerate(toks[e]):
            if rs and rs[-1][0] + rs[-1][1] == t:
                rs[-1] = (rs[-1][0], rs[-1][1] + 1, rs[-1][2])
            else:
                rs.append((t, 1, i))
        runs.append(rs)
    die = dies(tabs)
    own = [[] for _ in range(8)]
    load = [0] * 8
    load[RC] += len(runs[r])
    for group, par in ((SAME, 0), (OTHER, 1)):
        ds = [e for e in range(n) if e != r and (e + r) % 2 == par and toks[e]]
        for e in sorted(ds, key=lambda e: (-len(runs[e]), e)):
            pair = group[0:2] if die[(r, e)] == 1 else group[2:4]
            k = min(pair, key=lambda k: (load[k], k))
            own[k].append(e)
            load[k] += len(runs[e])
    cores = []
    for k in range(8):
        own[k].sort(key=lambda e: (e - r) % n)
        slots, units, base = [], [], 0
        for e in own[k]:
            s = len(slots)
            slots.append((e, "pack", base, len(toks[e])))
            units += [(s, t0, ln, "pack", base + i) for (t0, ln, i) in runs[e]]
            base += len(toks[e])
        if k == RC and toks[r]:
            s = len(slots)
            slots.append((r, "land", off[r][r], len(toks[r])))
            units += [(s, t0, ln, "land", off[r][r] + i) for (t0, ln, i) in runs[r]]
        assert base <= PACKW and len(slots) <= NSLOT
        cores.append({"slots": slots, "units": units, "xlist": [], "xcalls": [], "local": [], "tot": [0] * len(slots)})
    room = list(XROOM)
    left = []

    def space(o, t):
        return max(room[k] for k in range(8) if k != o and holds(k, t, 1))

    def hand(o, u):
        x = max((k for k in range(8) if k != o and holds(k, u[1], 1)),
                key=lambda k: (room[k] > 0 and (k != RC or RHOME[0] <= u[1] < RHOME[1]), room[k], -k))
        room[x] -= 1
        cores[x]["xlist"].append((o, u))

    for k in range(8):
        left.append([u for u in cores[k]["units"] if holds(k, u[1], u[2])])
    for i in range(max(len(c["units"]) for c in cores)):
        for k in range(8):
            us = cores[k]["units"]
            if i < len(us) and not holds(k, us[i][1], us[i][2]):
                for j in range(us[i][2]):
                    hand(k, (us[i][0], us[i][1] + j, 1, us[i][3], us[i][4] + j))
    while True:
        best = None
        for o in sorted(range(8), key=lambda k: (-len(left[k]) + LADJ[k], k)):
            ones = [u for u in left[o] if u[2] == 1]
            if ones:
                u = max(ones, key=lambda u: (space(o, u[1]), -u[0], -u[4]))
                if space(o, u[1]) > 0:
                    best = (o, u)
                    break
        if not best:
            break
        left[best[0]].remove(best[1])
        hand(best[0], best[1])
    for k in range(8):
        cores[k]["local"] = left[k]
        cores[k]["xlist"].sort(key=lambda p: (p[1][0], p[0]))
    for c in cores:
        xl = c["xlist"]
        for a in range(0, len(xl), 16):
            part = xl[a:a + 16]
            call = []
            for m, (o, (s, t0, ln, buf, col)) in zip(masks(len(part)), part):
                call.append((m, t0, o, buf, col, s))
                cores[o]["tot"][s] += bits(m)
            c["xcalls"].append(call)
    for c in cores:
        c["local"].sort(key=lambda u: (u[0], u[4]))
        for u in c["local"]:
            c["tot"][u[0]] += 16
    CACHE[key] = cores
    return cores


def rank_program(g, core, T, topo):
    k = core % 8
    base = core - k
    r = T.rank_of(base + RC)
    tabs = T.tables
    cnt, off = tables(tabs)
    n = len(cnt)
    me = chip_plan(r, tabs)[k]
    S = T.sem
    sent = 0

    parts = sorted(set(HOLD[h] for h in range(8) if h != RC))
    eng = 16 // len(parts)
    if k == RC:
        g.sync.dma_start(T.xs[:], T.x[:]).then_inc(S.ld, 16)
        ready, rval = S.ld, 16
        g.wait_ge(ready, rval)
        trs = []
        for i, (a, b) in enumerate(parts):
            ids = []
            for h in range(8):
                if h != RC and HOLD[h] == (a, b):
                    rid, pid = topo.addr(base + h, core)
                    ids.append(DstId(rid=rid, pnc=pid))
            trs.append(RemoteDMATransfer(dst_ids=ids, dma_engine_mask=((1 << eng) - 1) << (eng * i), remote_sem=S.xa,
                                         srcs=[T.xs[:, a:b]], dsts=[T.xs[:, a:b] for _ in ids]))
            sent += eng
        g.remote_dma_fused(trs, local_sem=S.sent)
    else:
        ready, rval = S.xa, eng
        g.wait_ge(ready, rval)
    g.sync.wait_ge(ready, rval)
    g.scalar.wait_ge(ready, rval)

    for call in me["xcalls"]:
        trs = []
        for (m, t, o, buf, col, s) in call:
            rid, pid = topo.addr(base + o, core)
            trs.append(RemoteDMATransfer(dst_ids=[DstId(rid=rid, pnc=pid)], dma_engine_mask=m,
                                         remote_sem=S["gh%d" % s], src=T.xs[:, t:t + 1], dst=T[buf][:, col:col + 1]))
            sent += bits(m)
        g.remote_dma_fused(trs, local_sem=S.sent)

    qs = (g.sync, g.scalar)
    for i, (s, t0, ln, buf, col) in enumerate(me["local"]):
        qs[i % 2].dma_start(T[buf][:, col:col + ln], T.xs[:, t0:t0 + ln]).then_inc(S["gh%d" % s], 16)

    for s, (e, buf, b, w) in enumerate(me["slots"]):
        if e == r:
            continue
        g.wait_ge(S["gh%d" % s], me["tot"][s])
        dst = T.cores[e]
        rid, pid = topo.addr(dst, core)
        m = topo.mask(core, dst)
        g.remote_dma(T.land[:, off[r][e]:off[r][e] + w], T.pack[:, b:b + w], S.arr, S.sent, pid, rid, m)
        sent += bits(m)
    g.wait_ge(S.sent, sent)

    if k == RC:
        g.sync.wait_ge(S.arr, 8 * sum(1 for q in range(n) if q != r and cnt[q][r]))
        for s, (e, buf, b, w) in enumerate(me["slots"]):
            if e == r:
                g.sync.wait_ge(S["gh%d" % s], me["tot"][s])
        width = sum(cnt[q][r] for q in range(n))
        g.sync.dma_start(T.y[:, 0:width], T.land[:, 0:width]).then_inc(S.st, 16)
        g.sync.wait_ge(S.st, 16)
